import numpy as np, ml_dtypes
CORES = [25,29,65,69,153,157,193,197]
N = 8
import mx_ref
BF = ml_dtypes.bfloat16
def gentries(a):
    return np.ascontiguousarray(a.reshape(8, 16, -1).transpose(0, 2, 1)).reshape(8, -1)
def gtable(e):
    e = np.asarray(e); return np.ascontiguousarray(e.reshape(8, -1, 16).transpose(0, 2, 1)).reshape(128, -1).astype(np.int32)
def gcols(t, e):
    v = np.concatenate([t.reshape(8, 16, -1, 4), np.zeros((8, 16, 1, 4), BF)], axis=2)
    return np.ascontiguousarray(np.stack([v[g][:, e[g]] for g in range(8)])).reshape(128, -1)
def tile(rs):
    return np.stack(rs, axis=2).reshape(128, -1).astype(BF)
def cut(t, i, w=512):
    return t[:, w * i:w * i + w]
def pick(q, e):
    c = np.concatenate([q[0].reshape(128, -1, 4), np.zeros((128, 1, 4), np.uint8)], axis=1); s = np.concatenate([q[1], np.ones((16, 1), np.uint8)], axis=1)
    return (np.ascontiguousarray(c[:, e].reshape(128, -1)), np.ascontiguousarray(s[:, e]))
def join(*qs):
    return (np.concatenate([q[0] for q in qs], axis=1), np.concatenate([q[1] for q in qs], axis=1))
def put(q, e, v):
    c, s = q[0].reshape(128, -1, 4).copy(), q[1].copy(); c[:, e] = v[0].reshape(128, -1, 4); s[:, e] = v[1]
    return (c.reshape(128, -1), s)
def pk(c, s):
    return (np.ascontiguousarray(c), mx_ref.live(s))
def emit(q):
    return q[0], q[1]
def packed(v, rng):
    q = [mx_ref.quantize(np.ascontiguousarray(v[r])) for r in range(N)]
    return np.stack([a for a, b in q]), np.stack([mx_ref.plane(b, rng) for a, b in q])
def values_of_codes():
    e, c = np.zeros((128, 128, 4), np.float32), np.zeros((128, 2, 4), np.uint8)
    e[np.arange(128), np.arange(128), 0] = 1
    c[:127, :, 0] = np.arange(256).reshape(2, 128).T[:127]
    return mx_ref.matmul(mx_ref.quantize(e.reshape(128, 512).astype(BF)), (c.reshape(128, 8), np.full((16, 2), 127, np.uint8))).T.reshape(-1).astype(np.float64)
CODE_VALUE, SCALE_VALUE = values_of_codes(), 2.0 ** (np.arange(256) - 127.0)
def decode(q):
    return (CODE_VALUE[q[0]].reshape(16, 8, -1, 4) * SCALE_VALUE[q[1]][:, None, :, None] + 0.0).reshape(128, -1).astype(np.float32)
def f(rng, *shape):
    return mx_ref.flush((rng.standard_normal(shape, dtype=np.float32) * np.exp2(rng.integers(-2, 3, shape[:-1] + (1,)))).astype(BF))
def wide(rng, *shape, cols=0):
    v = rng.standard_normal(shape, dtype=np.float32) * np.exp2(rng.integers(-12, 13, shape)).astype(np.float32)
    if cols: v *= np.repeat(np.exp2(rng.integers(-cols, cols + 1, shape[:-2] + (1, shape[-1] // 4))) * (rng.random(shape[:-2] + (1, shape[-1] // 4)) > 0.0625), 4, axis=-1).astype(np.float32)
    return mx_ref.flush(v.astype(BF))
M, P, K, L, A, R = 256, 256, 32, 128, 96, 3
def order(p):
    return np.argsort(-(p + np.float32(0.0)), axis=1, kind="stable")
def counts(e):
    return np.stack([np.bincount(e[g], minlength=M) for g in range(8)])
def gput(t, e, v):
    a, b = t.reshape(8, 16, -1, 4).copy(), v.reshape(8, 16, -1, 4)
    for g in range(8): a[g][:, e[g]] = b[g]
    return a.reshape(128, -1)
def big(v):
    v = v.astype(np.float32)
    v[np.abs(v) < np.float32(2.0 ** -16)] = 0
    return v.astype(BF)
def stored(l):
    return np.stack([gtable(e) for e in l])
def numbers_of(rng):
    return {"m": big(f(rng, N, 128, 4 * M)), "u": np.array(f(rng, N, 128, 512)), "v": np.array(f(rng, N, 128, 512)), "pt": stored(rng.integers(0, M, (N, 8, P)))}
def weights(rng, on=range(16), w=None):
    w = big(f(rng, N, 128, 2048)) if w is None else w
    w = w.reshape(N, 8, 16, 4, 8, 16, 4)
    for i in range(16):
        if i not in on:
            w[:, :, i] = 0
            w[:, :, :, :, :, i] = 0
    c, p = packed(w.reshape(N, 128, 2048), rng)
    return {"wc": c, "ws": p}
def signs(rng):
    return np.stack([rng.permutation(8) % 2 * 2.0 - 1.0 for r in range(N)])
def digits(rng, a, k, e):
    d = numbers_of(rng)
    x = d["m"].astype(np.float32).reshape(N, 8, 16, M, 4)
    s = np.arange(M) // 2
    b = ((s[:, None] >> np.arange(8)) & 1) * 2.0 ** (np.arange(8) - 23.0)
    x[:, :, 0] = 0
    x[:, :, 0, :, 0] = a[:, :, None]
    x[:, :, 8] = b[:, :4]
    x[:, :, 9] = b[:, 4:]
    x[:, :, 10:] = rng.integers(4, 8, (N, 8, 6, M, 4)) * rng.choice([-1.0, 1.0], (N, 8, 6, M, 4)) * 2.0 ** -20
    u = d["u"].reshape(N, 128, 128, 4)
    for g in range(8):
        u[:, :, 16 * g:16 * g + 2] = 0
        for j in range(2):
            u[:, 16 * g, 16 * g + j, 0] = k.astype(np.float32).astype(BF)
            u[:, 16 * g + 8:16 * g + 10, 16 * g + j] = (k * e[:, g] ** j).astype(np.float32).astype(BF)[:, None, None]
    d["m"] = x.reshape(N, 128, 4 * M).astype(BF)
    return d
def setup_inputs(rng):
    return {**numbers_of(rng), **weights(rng)}
def setup_inputs_ties(rng):
    d = numbers_of(rng)
    o = rng.permutation(N)
    x = d["m"].reshape(N, 8, 16, M, 4)
    u = d["u"].reshape(N, 8, 16, 128, 4)
    def small(*s):
        return (rng.integers(4, 8, s) * rng.choice([-1.0, 1.0], s) * 2.0 ** -30).astype(np.float32).astype(BF)
    for r in range(N):
        k = rng.permutation(M) % 3
        if o[r] == 0: k = np.zeros(M, int)
        if o[r] == 1: k = np.full(M, 2)
        a = x[r][:, :8, :3].copy()
        if o[r] % 2 == 0:
            a = small(8, 8, 3, 4)
            for j in range(2): u[r][:, :8, j::16] = small(8, 8, 8, 4)
            for g in rng.permutation(8)[:4]:
                a[g] = 0
                a[g, 0, :2, 0] = (np.array([1.0, -1.0]) * 2.0 ** -30).astype(np.float32).astype(BF)
                u[r, g, :8, 16 * g:16 * g + 2] = 0
                u[r, g, 0, 16 * g:16 * g + 2, 0] = (rng.choice([-1.0, 1.0], 2) * 2.0 ** -30).astype(np.float32).astype(BF)
        a[:, :, 2] = 0
        x[r][:, :8] = a[:, :, k]
    for g in range(8):
        e = u[:, g, :8, 16 * g:16 * g + 2].copy()
        u[:, :, :, 16 * g:16 * g + 2] = 0
        u[:, g, :8, 16 * g:16 * g + 2] = e
    return {**d, **weights(rng, range(8, 16))}
def setup_inputs_near(rng):
    l = np.sort(rng.integers(0, M, (N, 8, P)), axis=2)
    k = np.where(rng.permutation(N) < N // 2, 2.0 ** -30, 1.0)
    d = digits(rng, signs(rng), k, signs(rng))
    x = d["m"].reshape(N, 8, 16, M, 4)
    for r in range(N):
        for g in rng.permutation(8)[:4]: x[r, g, 0, l[r, g, rng.integers(P)], 0] = 2.0 ** 30
    return {**d, "pt": stored(l), **weights(rng, range(1, 8))}
def setup_inputs_shares(rng):
    o = rng.permutation(N)
    l = np.argsort(rng.random((N, 8, M)), axis=2)[:, :, :P]
    e = np.ones((N, 8))
    for r in range(N):
        if o[r] % 4 == 0: e[r] = -1
        if o[r] % 4 == 1: l[r] = l[r][:, :1].copy()
        if o[r] % 4 == 3: l[r] = l[r][:, rng.permutation(P) // 2]
    return {**digits(rng, np.ones((N, 8)), np.ones(N), e), "pt": stored(l), **weights(rng, range(1, 8))}
def setup_inputs_huge(rng):
    d = numbers_of(rng)
    o = rng.permutation(N)
    l = rng.integers(0, M, (N, 8, P))
    x = 2.0 ** 30 * (0.9 + 0.1 * rng.random((N, 8, 16, M, 4)))
    x[:, :, 15] = 2.0 ** 26 * rng.uniform(-1, 1, (N, 8, M, 4))
    for r in range(N):
        if o[r] % 2:
            c, s = rng.permutation(M) % 2, rng.permutation(P) % 2
            x[r][:, :15] *= (2.0 * c - 1.0)[:, None]
            e = np.stack([np.flatnonzero(c == i) for i in range(2)])
            l[r] = e[s[None, :], rng.integers(0, M // 2, (8, P))]
    u = d["u"].reshape(N, 128, 128, 4)
    for j in range(2):
        u[:, :, j::16] = (2.0 ** 30 * (0.9 + 0.1 * rng.random((N, 128, 8, 4))) * signs(rng)[:, None, :, None]).astype(np.float32).astype(BF)
        u[:, 15::16, j::16] = 0
    d["m"] = big(x.reshape(N, 128, 4 * M))
    return {**d, "pt": stored(l), **weights(rng, [15], rng.choice([-1.0, 1.0], (N, 128, 2048)).astype(np.float32).astype(BF))}
def setup_inputs_spread(rng):
    d = setup_inputs(rng)
    d["m"] = big(wide(rng, N, 128, 4 * M, cols=6))
    return d
def check_inputs(d):
    b = []
    for k in ("m", "u", "v"):
        a = np.abs(d[k].astype(np.float32))
        if not (np.isfinite(a).all() and ((a == 0) | (a >= 2.0 ** -30) & (a <= 2.0 ** 30)).all()): b.append("a value of " + k)
    if ((d["pt"] < 0) | (d["pt"] >= M)).any(): b.append("an entry of pt")
    if (d["wc"] % 128 == 127).any(): b.append("a code of wc that is no number")
    return b
def reference(m, u, v, pt, wc, ws):
    qu = [mx_ref.quantize(u[r]) for r in range(N)]
    lay = [pk(wc[r], ws[r]) for r in range(N)]
    pages = [m[r] for r in range(N)]
    now = [gentries(pt[r]).astype(np.int64) for r in range(N)]
    for t in range(R):
        o, wr, sent = [], [], []
        for r in range(N):
            one = gcols(pages[r], now[r])
            s = mx_ref.matmul(qu[r], mx_ref.quantize(one))
            o.append(order(s[::16]))
            wr.append(order(s[1::16])[:, :A])
            sent.append(mx_ref.quantize(gcols(one, o[r][:, :K])))
        came = decode(join(*sent)).astype(BF)
        for r in range(N):
            h = now[r].copy()
            free = np.argsort(counts(np.take_along_axis(h, o[r][:, :P - L], axis=1)) > 0, axis=1, kind="stable")
            p = gput(pages[r], free[:, :K], cut(came, (r - 1) % N, 4 * K))
            np.put_along_axis(h, o[r][:, P - L:], free[:, np.arange(L) % K], axis=1)
            at = np.take_along_axis(h, wr[r], axis=1)
            more = np.take_along_axis(counts(h), at, axis=1) > 1
            z = gcols(p, at)
            q = mx_ref.quantize(z)
            made = tile([np.maximum(mx_ref.matmul(pick(lay[r], np.arange(128 * b, 128 * b + 128)), q), np.float32(0.0)) * np.float32(0.03125) + z[:, b::4].astype(np.float32) for b in range(4)])
            i = np.argsort(np.argsort(~more, axis=1, kind="stable"), axis=1)
            to = np.where(more, np.take_along_axis(free, K + i, axis=1), at)
            np.put_along_axis(h, wr[r], to, axis=1)
            pages[r] = gput(p, to, made)
            now[r] = h
    y, om = np.zeros((N, 128, P), np.float32), np.zeros((N, 8, P), np.float32)
    oc, osc = np.zeros((N, 128, 4 * P), np.uint8), np.zeros((N, 16, P), np.uint8)
    for r in range(N):
        q = mx_ref.quantize(gcols(pages[r], now[r]))
        y[r] = mx_ref.matmul(mx_ref.quantize(v[r]), q)
        om[r] = now[r]
        oc[r], osc[r] = emit(q)
    return {"y": y, "om": om, "oc": oc, "osc": osc}

@@ -1,0 +1,609 @@
+from concourse.mybir import dt, AluOpType, AxisListType, ActivationFunctionType
+
+R, P, K, A = 3, 256, 32, 96
+ROWS = [[9, 10], [9, 10], [9, 10]]
+AM = 14
+SEED, SLACK, SAME, CROSS, RING = 1, 0, 60, 100, 6000.0
+URGE = [-42e3, -42e3, 137e3, 142e3, -38e3, 37e3, 371e3, -179e3, 128e3, 500.0, 5500.0, -256e3, -52e3, -163e3]
+TRIES, LEAN = 2500, 0.6
+DS, HS = 256, 352
+WN = HS + A
+BIG = 1e29
+HOLD = 1024.0
+BF, F16, F32, I32, U16, CODE, U8 = "bfloat16", "float16", "float32", "int32", "uint16", "float8_e4m3fn_x4", "uint8"
+FLW, SCW = 256 * (AM + 1), 128 * (AM + 1) + 16
+
+
+def _sb(n, d):
+    return ("sbuf", [128, n], d)
+
+
+SCRATCH = {
+    "M0": _sb(1024, BF), "UT": _sb(512, BF), "VT": _sb(512, BF), "PT": _sb(16, I32),
+    "WC": _sb(512, CODE), "WS": _sb(512, U8), "UQ": _sb(128, CODE), "US": _sb(128, U8),
+    "UP": _sb(256, CODE), "UPS": _sb(256, U8), "VQ": _sb(128, CODE), "VS": _sb(128, U8),
+    "ET": _sb(2048, BF), "EQ": _sb(512, CODE), "ES": _sb(512, U8), "ZERO": _sb(896, BF),
+    "WA": _sb(4 * WN, BF), "WB": _sb(4 * WN, BF), "FQ": _sb(256 * 4, CODE), "FS": _sb(256 * 4, U8),
+    "BT": _sb(512, BF), "BQ": _sb(128 * R, CODE), "BS": _sb(128 * R, U8),
+    "LC": _sb(608, CODE), "LS": _sb(608, U8), "RC": _sb(32 * R, CODE), "RS": _sb(32 * R, U8),
+    "ZT": _sb(512, BF), "ZQ": _sb(128, CODE), "ZS": _sb(128, U8), "RB": _sb(4 * A, F32),
+    "IOF": _sb(HS, F32), "IOB": _sb(256, BF), "IOP": _sb(256, BF), "N16": _sb(256, F32), "CI": _sb(24, I32),
+    "CF": _sb(176, F32), "UL": _sb(16, U16), "MK": _sb(256, F32), "DM": _sb(256, F32),
+    "KH": _sb(256, F32), "KX": _sb(384, BF),
+    "ZZ": _sb(1024, F32), "TA": _sb(512, F32), "D1": _sb(512, F32), "HF": _sb(512, F32),
+    "FL": _sb(2 * FLW, F16), "SC": _sb(2 * SCW, F16), "SG": _sb(2 * 4096, BF),
+    "RI": _sb(32 * R, I32), "SM": _sb(512 * R, F32), "LI": _sb(192 * R + 64, U16),
+    "OF": _sb(256, BF), "OM": _sb(128, F16), "S1": _sb(256, F32), "ZF": _sb(256, F32), "ZM": _sb(A, F32),
+    "TW": _sb(2 * WN, BF), "WT": _sb(768 * R, BF), "TL": _sb(128, BF), "HJ": _sb(17 * 128, BF),
+    "TB": _sb(3 * A, BF), "TF": _sb(4 * A, F32), "TO": _sb(256, F32), "YS": _sb(256, F32),
+    "P0": ("psum", [128, 512], F32), "P1": ("psum", [128, 512], F32), "P2": ("psum", [128, 512], F32),
+    "P3": ("psum", [128, 512], F32), "P4": ("psum", [128, 512], F32), "P5": ("psum", [128, 512], F32),
+}
+SEMAPHORES = (["v", "a", "t", "g", "st", "sent"] + ["d%d" % i for i in range(16)]
+              + ["ac%d" % r for r in range(R)] + ["as%d" % r for r in range(R)])
+PLAN = {}
+
+
+def _mask(es):
+    m = 0
+    for e in es:
+        m |= 1 << e
+    return m
+
+
+def _halves(topo, a, b):
+    es = topo.engines(a, b)
+    h = len(es) // 2
+    return es[:h], es[h:]
+
+
+def _relay(topo, cores, a, b):
+    if topo.may_write(a, b):
+        return None
+    c = [x for x in topo.cores_of(a) if x not in cores and topo.may_write(x, b)]
+    c.sort(key=lambda x: topo.die(x) != topo.die(a))
+    return c[0]
+
+
+def _overlap(x, y):
+    if x[0] != y[0] or x[1] >= y[2] or y[1] >= x[2]:
+        return False
+    if x[3] == y[3] and x[3] > 1 and (x[1] - y[1]) % x[3]:
+        return False
+    return True
+
+
+def _deps(ops):
+    out = []
+    for i, o in enumerate(ops):
+        d = set(o["after"])
+        for j in range(i):
+            p = ops[j]
+            hit = False
+            for w in p["w"]:
+                if any(_overlap(w, x) for x in o["r"]) or any(_overlap(w, x) for x in o["w"]):
+                    hit = True
+            for x in p["r"]:
+                if any(_overlap(x, w) for w in o["w"]):
+                    hit = True
+                if SCRATCH[x[0]][0] == "psum" and any(y[0] == x[0] for y in o["r"]) and \
+                        (len(p["ways"]) > 1 or len(o["ways"]) > 1 or p["ways"][0][0] != o["ways"][0][0]):
+                    hit = True
+            if hit:
+                d.add(j)
+        out.append(d)
+    return out
+
+
+def _schedule(ops, deps, succ, bonus, lean, slack):
+    n = len(ops)
+    pr = [0.0] * n
+    for i in range(n - 1, -1, -1):
+        pr[i] = ops[i]["least"] + max([pr[j] + 80 for j in succ[i]] + [0.0])
+    pr = [p + b for p, b in zip(pr, bonus)]
+    left = [len(d) for d in deps]
+    free, end, at, way, order, on = {}, [0.0] * n, [0.0] * n, [0] * n, [], [""] * n
+    ready = {i: [0.0] * len(ops[i]["ways"]) for i in range(n) if not left[i]}
+    while ready:
+        cand = []
+        for i, t in ready.items():
+            pick = None
+            for k, w in enumerate(ops[i]["ways"]):
+                s = max(free.get(w[0], 0.0), t[k])
+                e = s + w[1] + (lean[i] if k == 0 else 0.0)
+                if pick is None or e < pick[0]:
+                    pick = (e, s, k, w[0])
+            cand.append((pick[1], i, pick[2], pick[3]))
+        first = min(cand)
+        s, i, k, _ = max([c for c in cand if c[3] == first[3] and c[0] <= first[0] + slack], key=lambda c: pr[c[1]])
+        del ready[i]
+        w = ops[i]["ways"][k]
+        free[w[0]] = s + w[1]
+        end[i], at[i], way[i], on[i] = s + w[1] + ops[i]["lat"], s, k, w[0]
+        order.append(i)
+        for j in succ[i]:
+            left[j] -= 1
+            if not left[j]:
+                ready[j] = [max(end[d] + (SAME if on[d] == u[0] else CROSS) for d in deps[j]) for u in ops[j]["ways"]]
+    return max(end), order, way, at
+
+
+def _plan(ops):
+    if "p" not in PLAN:
+        deps = _deps(ops)
+        n = len(ops)
+        succ = [[] for _ in ops]
+        for i in range(n):
+            ops[i]["least"] = min(w[1] for w in ops[i]["ways"]) + ops[i]["lat"]
+            for j in deps[i]:
+                succ[j].append(i)
+        both = [i for i in range(n) if len(ops[i]["ways"]) > 1]
+        bonus, lean, slack = [URGE[o["kin"]] for o in ops], [LEAN * o["ways"][0][1] for o in ops], SLACK
+        best = _schedule(ops, deps, succ, bonus, lean, slack)
+        now = best[0]
+        x = [SEED]
+
+        def draw(m):
+            x[0] = (x[0] * 1103515245 + 12345) % 2147483648
+            return (x[0] >> 8) % m
+
+        for t in range(TRIES):
+            b, le, sl = list(bonus), list(lean), slack
+            for _ in range(draw(4)):
+                i, d = draw(n), draw(12001) - 6000.0
+                for j in range(i, min(n, i + 1 + draw(10))):
+                    b[j] += d
+            if draw(3) == 0:
+                k, d, lo = draw(len(URGE)), draw(12001) - 6000.0, draw(3 * n) - 2 * n
+                hi = lo + n // 3 if lo > 0 else n
+                for j in range(max(lo, 0), min(hi, n)):
+                    if ops[j]["kin"] == k:
+                        b[j] += d
+            for _ in range(draw(3)):
+                le[both[draw(len(both))]] = (-3000.0, 0.0, 300.0, 3000.0)[draw(4)]
+            if draw(12) == 0:
+                sl = 40 * draw(8)
+            s = _schedule(ops, deps, succ, b, le, sl)
+            if s[0] <= now + 150.0 * (1.0 - t / TRIES):
+                now, bonus, lean, slack = s[0], b, le, sl
+                if s[0] < best[0]:
+                    best = s
+        PLAN["p"] = (deps, best)
+    return PLAN["p"]
+
+
+def _calls(g, T, to, topo, core, land):
+    Op, Fn = AluOpType, ActivationFunctionType
+    ops = []
+    nd = [0]
+    kin = [0]
+
+    def v(name, lo, hi, st=1):
+        return (name, lo, hi, st)
+
+    def ap(x):
+        if isinstance(x, tuple) and x[0] == "ind":
+            return ap(x[1]).indirect(ap(x[2]))
+        if isinstance(x, tuple):
+            return T[x[0]][:, x[1]:x[2]:x[3]] if x[3] > 1 else T[x[0]][:, x[1]:x[2]]
+        return x
+
+    def ind(w, o):
+        return ("ind", w, o)
+
+    def regs(*xs):
+        out = []
+        for x in xs:
+            if isinstance(x, tuple):
+                out += [x[1], x[2]] if x[0] == "ind" else [x]
+        return out
+
+    def size(x):
+        return 16 * size(x[2]) if x[0] == "ind" else (x[2] - x[1] + x[3] - 1) // x[3]
+
+    def two(*xs):
+        return all(x[0] != "ind" and SCRATCH[x[0]][2] in (BF, F16, U16) for x in xs)
+
+    def add(q, cost, r, w, emit, lat=0.0, kind="c", after=()):
+        ops.append({"ways": [(q, cost, emit)], "lat": lat, "r": r, "w": w, "kind": kind, "after": list(after),
+                    "kin": kin[0]})
+        return len(ops) - 1
+
+    def either():
+        o = ops.pop()
+        ops[-1]["ways"] += o["ways"]
+        ops[-1]["r"] = ops[-1]["r"] + o["r"]
+
+    def rate(o, x):
+        return 1.56 if x[0] == "ind" else 0.5 if two(o, x) else 1.0
+
+    def ts(o, x, s1, op0, s2=None, op1=None):
+        def e():
+            if op1 is None:
+                return g.vector.tensor_scalar(ap(o), ap(x), ap(s1), None, op0)
+            return g.vector.tensor_scalar(ap(o), ap(x), ap(s1), ap(s2), op0, op1)
+        add("v", 55 + size(o) * rate(o, x), regs(x, s1, s2), [o], e)
+
+    def tt(o, x, y, op):
+        k = 1.0 if SCRATCH[x[0]][0] == "psum" else 2.0
+        add("v", 55 + size(o) * k, regs(x, y), [o], lambda: g.vector.tensor_tensor(ap(o), ap(x), ap(y), op))
+
+    def cp(o, x):
+        if o[0] == "ind":
+            add("v", 55 + size(x) * 3.8, [x, o[2]], [o[1]], lambda: g.vector.tensor_copy(ap(o), ap(x)))
+        else:
+            add("v", 55 + size(o) * rate(o, x), regs(x), [o], lambda: g.vector.tensor_copy(ap(o), ap(x)))
+
+    def scan(o, d0, d1, op0, op1):
+        add("v", 55 + size(o) * (0.5 if two(o, d0, d1) else 1.0), [d0, d1], [o],
+            lambda: g.vector.tensor_tensor_scan(ap(o), ap(d0), ap(d1), 0.0, op0, op1))
+
+    def hold(o, x):
+        scan(o, v("KX", 0, size(x)), x, Op.add, Op.max)
+
+    def fill(o, c):
+        add("v", 55 + size(o) * (0.5 if two(o) else 1.0), [], [o], lambda: g.vector.memset(ap(o), c))
+
+    def act(o, x, f, bias=None, scale=None, acc=None):
+        def e():
+            kw = {}
+            if bias is not None:
+                kw["bias"] = ap(bias)
+            if scale is not None:
+                kw["scale"] = scale
+            if acc is not None:
+                kw["accum_out"] = ap(acc)
+            return g.scalar.activation(ap(o), ap(x), f, **kw)
+        add("a", 70 + (20 if acc else 0) + size(o) * (1.56 if x[0] == "ind" else 1.0), regs(x, bias),
+            [o] + ([acc] if acc else []), e)
+
+    def move(o, x):
+        cp(o, x)
+        act(o, x, Fn.Copy)
+        either()
+
+    def line(o, x, a, b, relu=False):
+        if relu:
+            ts(o, x, 0.0, Op.max, a, Op.mult)
+        else:
+            ts(o, x, a, Op.mult, b, Op.add)
+        act(o, x, Fn.Relu if relu else Fn.Identity, bias=None if relu else b, scale=a)
+        either()
+
+    def quant(c, s, x):
+        add("v", 30 + size(x) * 0.27, [x], [c, s], lambda: g.vector.quantize_mx(ap(c), ap(s), ap(x)))
+
+    def mm(o, parts):
+        def e():
+            ins = None
+            for i, (a, b, c, d) in enumerate(parts):
+                ins = g.tensor.matmul_mx(ap(o), ap(a), ap(b), ap(c), ap(d), i == 0, i == len(parts) - 1)
+            return ins
+        add("t", len(parts) * (size(o) + 16) * 0.65, [x for p in parts for x in p], [v(o[0], 0, 512)], e, lat=100.0)
+
+    def iota(o, pat, base=0, cm=0):
+        def e():
+            if SCRATCH[o[0]][2] == I32:
+                return g.iota(ap(o), pat, base, cm)
+            return g.iota(ap(o), pat, base, cm, allow_small_or_imprecise_dtypes=True)
+        add("g", 150 + 2 * size(o), [], [o], e)
+
+    def dma(q, out, in_, r, w, lat, sem=None):
+        if sem is None:
+            sem = "d%d" % nd[0]
+            nd[0] += 1
+        eng = g.sync if q == "s" else g.scalar
+        i = add(q, 80, r, w, lambda: eng.dma_start(out(), in_()), lat=lat, kind="d")
+        ops[i]["sem"] = sem
+
+    def u8(x):
+        return ap(x).bitcast(dt.uint8)
+
+    dma("s", lambda: T.M0[:], lambda: T.m[:], [], [v("M0", 0, 1024)], 2600)
+    dma("a", lambda: T.PT[:], lambda: T.pt[:], [], [v("PT", 0, 16)], 2000)
+    dma("a", lambda: T.UT[:], lambda: T.u[:], [], [v("UT", 0, 512)], 2400)
+    dma("s", lambda: T.WC[:].bitcast(dt.uint8), lambda: T.wc[:], [], [v("WC", 0, 512)], 3000)
+    dma("s", lambda: T.WS[:], lambda: T.ws[:], [], [v("WS", 0, 512)], 3000)
+    dma("s", lambda: T.VT[:], lambda: T.v[:], [], [v("VT", 0, 512)], 3000)
+    fill(v("ZERO", 0, 896), 0.0)
+    for x in [v("TW", 0, 2 * WN), v("BT", 128, 512), v("ZT", 4 * A, 512), v("WA", 1024, 4 * WN), v("WB", 1024, 4 * WN)] + \
+            [v("WT", 768 * r, 768 * r + 768) for r in range(R)]:
+        z = v("ZERO", 0, size(x))
+        dma("s", lambda x=x: ap(x), lambda z=z: ap(z), [z], [x], 2500)
+    iota(v("CI", 0, 1), [[0, 1]], 0, 1)
+    iota(v("N16", 0, 256), [[0, 16], [1, 16]])
+    iota(v("CI", 8, 24), [[1, 2], [16, 8]])
+    iota(v("IOF", 0, HS), [[1, HS]])
+    iota(v("IOB", 0, 256), [[1, 256]])
+    iota(v("IOP", 0, 256), [[1, 16], [16, 16]], 1)
+    for h in range(4):
+        x = v("ET", 512 * h, 512 * h + 512)
+        iota(x, [[0, 512]], 1)
+        add("g", 170 + 1024, [x], [x], lambda x=x, h=h: g.affine_select(
+            ap(x), ap(x), [[-4, 128], [-1, 4]], Op.is_equal, 0.0, h, 4))
+    ts(v("CI", 1, 2), v("CI", 0, 1), 15, Op.bitwise_and)
+    ts(v("CI", 2, 3), v("CI", 0, 1), 31, Op.bitwise_and)
+    cp(v("CF", 0, 2), v("CI", 1, 3))
+    q, p32, q16, top, q1, hq = [v("CF", i, i + 1) for i in range(6)]
+    JW, THR, C256, M32 = v("CF", 8, 24), 24, v("CF", 48, 64), v("CF", 64, 96)
+    HT, h256, h255, h31 = 160, v("CF", 164, 165), v("CF", 165, 166), v("CF", 166, 167)
+    cp(v("UL", 0, 16), v("CI", 8, 24))
+    ts(v("MK", 0, 256), v("N16", 0, 256), q, Op.is_equal)
+    line(v("DM", 0, 256), v("MK", 0, 256), -2 * BIG, BIG)
+    line(v("KH", 0, 256), v("MK", 0, 256), 3 * BIG, 0.0)
+    fill(v("KH", 0, 256, 16), 3 * BIG)
+    for o in range(2):
+        cp(v("SC", SCW * o, SCW * o + 1), v("ZERO", 0, 1))
+    line(q1, q, 1.0, 1.0)
+    ts(hq, q, 15.0, Op.is_lt, -HOLD, Op.mult)
+    ts(v("KX", 128, 256), v("N16", 0, 128), q1, Op.is_equal, HOLD, Op.mult)
+    line(v("KX", 256, 384), v("MK", 0, 128), -4 * HOLD, 0.0)
+    tt(v("KX", 0, 128), v("KX", 128, 256), v("KX", 256, 384), Op.add)
+    line(v("CF", 7, 8), hq, 4.0, 0.0)
+    line(v("CF", HT, HT + 4), v("IOF", 0, 4), 1.0, v("CF", 7, 8))
+    line(h256, hq, -1.0, 256.0)
+    line(h255, hq, 1.0, 255.0)
+    line(h31, hq, 1.0, 31.0)
+    line(q16, q, -16.0, -0.5)
+    ts(top, p32, q, Op.subtract, 15.0, Op.add)
+    ts(JW, v("IOF", 0, 256, 16), q, Op.add, -float(HS), Op.add)
+    line(v("CF", THR, THR + 17), v("IOF", 0, 17), -1.0, q16)
+    line(C256, v("CF", THR, THR + 16), -1.0, 255.5)
+    ts(v("CF", 96, 128), v("IOF", 0, 32), p32, Op.is_gt)
+    ts(v("CF", 128, 160), v("IOF", 0, 32), top, Op.is_le)
+    tt(M32, v("CF", 96, 128), v("CF", 128, 160), Op.mult)
+    for r in range(R + 1):
+        quant(v("LC", 160 * r, 160 * r + 128), v("LS", 160 * r, 160 * r + 128), v("ZERO", 0, 512))
+    quant(v("EQ", 0, 512), v("ES", 0, 512), v("ET", 0, 2048))
+    quant(v("UQ", 0, 128), v("US", 0, 128), v("UT", 0, 512))
+    ul = v("UL", 0, 16)
+    add("v", 455, [v("UQ", 0, 128), ul], [v("UP", 0, 256)], lambda: g.vector.tensor_copy(
+        T.UP[:, 0:256].bitcast(dt.uint32), T.UQ[:, 0:128].bitcast(dt.uint32).indirect(ap(ul))))
+    move(v("UPS", 0, 256), ind(v("US", 0, 128), ul))
+    quant(v("VQ", 0, 128), v("VS", 0, 128), v("VT", 0, 512))
+    l0 = 192 * R
+    for t in range(4):
+        ts(v("LI", l0 + 16 * t, l0 + 16 * t + 16), v("PT", 0, 16), 4.0, Op.mult, float(t), Op.add)
+        move(v("WA", t, 1024, 4), ind(v("M0", 0, 1024), v("LI", l0 + 16 * t, l0 + 16 * t + 16)))
+    p16 = v("LI", 192 * (R - 1) + 176, 192 * R)
+    kin[0] = 1
+    cp(p16, v("PT", 0, 16))
+    line(v("TW", 0, 256), ind(v("IOF", 0, 256), p16), 1.0, 1.0)
+
+    def ranks(r, o, out):
+        a = ROWS[r][o]
+        kin[0] = 4 + 3 * o
+        pv, pa = v("P%d" % (2 * o), 0, 256), v("P%d" % (2 * o + 1), 0, 256)
+        side = (v("UP", 128 * o, 128 * o + 128), v("UPS", 128 * o, 128 * o + 128),
+                v("FQ", 256 * r, 256 * r + 256), v("FS", 256 * r, 256 * r + 256))
+        mm(pa, [side])
+        mm(pv, [side])
+        z, b, fl, sc = 512 * o, 256 * o, FLW * o, SCW * o
+        hf = v("HF", b, b + 256)
+        act(v("TA", b, b + 256), pa, Fn.Abs, bias=2.0 ** -125, scale=1.0625 * 2.0 ** -24)
+        act(v("ZZ", z + 16, z + 256), v(pa[0], 16, 256), Fn.Copy)
+        tt(v("D1", b, b + 256), pv, v("DM", 0, 256), Op.max)
+        scan(hf, v("KH", 0, 256), v("D1", b, b + 256), Op.add, Op.min)
+        tt(v("ZZ", z + 256, z + 512), pv, v("TA", b, b + 256), Op.add)
+        tt(v("FL", fl, fl + 256), pv, hf, Op.is_equal)
+        acc = 512 * r + 16 * o
+        kin[0] += 1
+        for c in range(16):
+            win, s = v("ZZ", z + 16 * c + 16, z + 16 * c + 272), v("HF", b + 16 * c + 15, b + 16 * c + 16)
+            if c < a:
+                ts(v("FL", fl + 256 * (c + 1), fl + 256 * (c + 2)), win, s, Op.is_gt, -0.5, Op.add)
+            else:
+                sg = v("SG", 4096 * o + 256 * c, 4096 * o + 256 * c + 256)
+                act(sg, win, Fn.Sign, bias=s, scale=-1.0)
+                act(sg, sg, Fn.Relu, scale=-1.0, acc=v("SM", acc + c, acc + c + 1))
+        w = 128 * (a + 1)
+        kin[0] += 1
+        scan(v("SC", sc + 1, sc + 1 + w), v("FL", fl, fl + 2 * w, 2), v("FL", fl + 1, fl + 2 * w, 2), Op.add, Op.add)
+        d1, d2 = v("SM", 512 * r + 400 + 32 * o, 512 * r + 416 + 32 * o), v("SM", 512 * r + 416 + 32 * o, 512 * r + 416 + 32 * o + a)
+        tt(d1, v("SC", sc + 8, sc + 129, 8), v("SC", sc, sc + 121, 8), Op.subtract)
+        tt(d2, v("SC", sc + 256, sc + w + 1, 128), v("SC", sc + 128, sc + w - 127, 128), Op.subtract)
+        line(v("SM", acc, acc + a), d2, 1.0, 128.0)
+        tt(out, v("SM", acc, acc + 16), d1, Op.subtract)
+
+    sends = []
+    for r in range(R):
+        W, Wn = ("WA", "WB") if r % 2 == 0 else ("WB", "WA")
+        tw, tn = WN * (r % 2), WN * (1 - r % 2)
+        li, sm, ri, wt = 192 * r, 512 * r + 32, 32 * r, 768 * r
+
+        def L(a, n):
+            return v("LI", li + a, li + a + n)
+
+        def S(a, n):
+            return v("SM", sm + a, sm + a + n)
+
+        kin[0] = 10
+        quant(v("FQ", 256 * r, 256 * r + 256), v("FS", 256 * r, 256 * r + 256), v(W, 0, 1024))
+        rho, alp = v("RI", ri, ri + 16), S(432, 16)
+        ranks(r, 0, rho)
+        cp(L(0, 16), rho)
+        cp(ind(v("OF", 0, 256), L(0, 16)), v("IOB", 0, 256))
+        hold(v("OM", 0, 128), v("OF", 0, 128))
+        for t in range(4):
+            ts(L(16 + 2 * t, 2), v("OM", 15, 32, 16), 4.0, Op.mult, v("CF", HT + t, HT + t + 1), Op.add)
+            move(v("BT", t, 128, 4), ind(v(W, 0, 1024), L(16 + 2 * t, 2)))
+        bq, bs = v("BQ", 128 * r, 128 * r + 128), v("BS", 128 * r, 128 * r + 128)
+        quant(bq, bs, v("BT", 0, 512))
+        rid, pid = topo.addr(to, core)
+        e0, e1 = _halves(topo, core, to)
+        lc, ls = v("LC", 160 * r + 128, 160 * r + 160), v("LS", 160 * r + 128, 160 * r + 160)
+        oc_, os_ = (lc, ls) if land else (v("RC", 32 * r, 32 * r + 32), v("RS", 32 * r, 32 * r + 32))
+        bc, bp = v("BQ", 128 * r, 128 * r + 32), v("BS", 128 * r, 128 * r + 32)
+        s0 = add("g", 300, [bc], [], lambda r=r, o=oc_, x=bc, m=_mask(e0): g.remote_dma(
+            u8(o), u8(x), T.sem["ac%d" % r], T.sem.sent, pid, rid, m), kind="r")
+        s1 = add("g", 300, [bp], [], lambda r=r, o=os_, x=bp, m=_mask(e1): g.remote_dma(
+            ap(o), ap(x), T.sem["as%d" % r], T.sem.sent, pid, rid, m), kind="r", after=[s0])
+        sends.append(len(e0) + len(e1))
+        i = add("n", 0, [], [lc, ls], None, lat=RING, kind="n", after=[s0, s1])
+        ops[i]["round"] = r
+        kin[0] = 2
+        ts(L(24, 8), v("OM", 15, 128, 16), hq, Op.add)
+        move(v("TL", 0, 128), ind(v("TW", tw, tw + 256), L(24, 8)))
+        kin[0] = 3
+        ts(v("RI", ri + 16, ri + 32), rho, 159, Op.bitwise_and)
+        ts(S(0, 16), v("RI", ri + 16, ri + 32), 3.0, Op.mult, -128.0 - HS, Op.add)
+        tt(S(16, 16), S(0, 16), JW, Op.max)
+        ts(L(32, 16), S(16, 16), float(HS), Op.add)
+        move(v("S1", 0, 256), ind(v("IOF", 0, HS), L(32, 16)))
+        ranks(r, 1, alp)
+        cp(L(48, 16), alp)
+        cp(ind(v("ZF", 0, 256), L(48, 16)), v("S1", 0, 256))
+        hold(v("ZM", 0, A), v("ZF", 0, A))
+        zw = v("ZM", 15, A, 16)
+        ts(S(32, 16), alp, float(A), Op.is_ge, 1000.0, Op.mult)
+        act(S(32, 16), alp, Fn.Relu, bias=-1000.0 * (A - 1), scale=1000.0)
+        either()
+        tt(S(48, 16), alp, S(32, 16), Op.subtract)
+        tt(S(64, 16), S(48, 16), S(16, 16), Op.max)
+        kin[0] = 10
+        mm(v("P4", 0, 128), [(v("EQ", 128 * b, 128 * b + 128), v("ES", 128 * b, 128 * b + 128),
+                              v("LC", 160 * r + 128 - 32 * b, 160 * r + 256 - 32 * b),
+                              v("LS", 160 * r + 128 - 32 * b, 160 * r + 256 - 32 * b)) for b in range(4)])
+        for b in range(4):
+            act(v(W, 4 * DS + b, 4 * HS, 12), v("P4", 32 * b, 32 * b + 32), Fn.Copy)
+        for t in range(4):
+            ts(L(64 + 6 * t, 6), zw, 4.0, Op.mult, v("CF", HT + t, HT + t + 1), Op.add)
+            move(v("ZT", t, 4 * A, 4), ind(v(W, 0, 4 * HS), L(64 + 6 * t, 6)))
+        quant(v("ZQ", 0, 128), v("ZS", 0, 128), v("ZT", 0, 512))
+        for b in range(4):
+            mm(v("P%d" % b, 0, 128), [(v("WC", 128 * b, 128 * b + 128), v("WS", 128 * b, 128 * b + 128),
+                                       v("ZQ", 0, 128), v("ZS", 0, 128))])
+            line(v("RB", A * b, A * b + A), v("P%d" % b, 0, A), 0.03125, 0.0, relu=True)
+            tt(v(W, 4 * HS + b, 4 * WN, 4), v("RB", A * b, A * b + A), v("ZT", b, 4 * A, 4), Op.add)
+        for t in range(4):
+            ts(L(96 + 16 * t, 16), S(64, 16), 4.0, Op.mult, float(t + 4 * HS), Op.add)
+            move(v(Wn, t, 1024, 4), ind(v(W, 0, 4 * WN), L(96 + 16 * t, 16)))
+        kin[0] = 11
+        for c in range(17):
+            act(v("HJ", 128 * c, 128 * c + 128), v("TL", 0, 128), Fn.Sign, bias=v("CF", THR + c, THR + c + 1), acc=S(80 + c, 1))
+        cnt = S(112, 16)
+        kin[0] = 12
+        tt(cnt, S(80, 16), S(81, 16), Op.subtract)
+        ts(S(128, 16), cnt, 0.0, Op.is_equal)
+        act(S(128, 16), cnt, Fn.Relu, bias=1.0, scale=-1.0)
+        either()
+        scan(S(144, 16), v("IOF", 0, 16), S(128, 16), Op.min, Op.add)
+        ts(S(160, 32), M32, S(159, 1), Op.mult)
+        add("v", 90, [S(160, 32)], [S(192, 32)], lambda a=S(192, 32), b=S(160, 32): g.vector.transpose(ap(a), ap(b)))
+        add("v", 90, [S(192, 32)], [S(224, 1)], lambda a=S(224, 1), b=S(192, 32): g.vector.tensor_reduce(
+            ap(a), ap(b), AxisListType.X, Op.add))
+        line(S(248, 16), cnt, 1000.0, -1.0)
+        tt(S(232, 16), S(144, 16), S(248, 16), Op.add)
+        line(S(264, 16), S(232, 16), 1.0, S(224, 1))
+        act(S(280, 16), cnt, Fn.Relu, bias=512.0, scale=-128.0)
+        tt(S(296, 16), S(280, 16), C256, Op.add)
+        tt(S(312, 16), S(264, 16), S(296, 16), Op.min)
+        cp(L(160, 16), S(312, 16))
+        pages = v("WT", wt, wt + 768)
+        cp(ind(pages, L(160, 16)), v("IOP", 0, 256))
+        kin[0] = 13
+        ts(L(88, 6), zw, hq, Op.add)
+        move(v("TB", 0, A), ind(v("TW", tw, tw + HS), L(88, 6)))
+        hold(v("TF", 0, A), v("TB", 0, A))
+        at = v("TF", 15, A, 16)
+        ts(S(328, 6), zw, h256, Op.is_ge, -1000.0, Op.mult)
+        tt(S(336, 6), S(328, 6), at, Op.add)
+        ts(L(176, 6), S(336, 6), h255, Op.add, 0.0, Op.max)
+        more = v("TB", A, 2 * A)
+        ts(more, ind(pages, L(176, 6)), 0.0, Op.is_gt)
+        act(more, ind(pages, L(176, 6)), Fn.Sign)
+        either()
+        scan(v("TB", 2 * A, 3 * A), v("IOB", 0, A), more, Op.min, Op.add)
+        line(v("TF", A, 2 * A), more, -800.0, 800.0)
+        tt(v("TF", 2 * A, 3 * A), v("TF", A, 2 * A), v("TB", 2 * A, 3 * A), Op.add)
+        hold(v("TF", 3 * A, 4 * A), v("TF", 2 * A, 3 * A))
+        line(S(344, 6), at, 1.0, 480.0)
+        tt(S(352, 6), S(344, 6), v("TF", 3 * A + 15, 4 * A, 16), Op.min)
+        ts(L(182, 6), S(352, 6), h31, Op.add)
+        move(v("TW", tw + HS, tw + WN), ind(pages, L(182, 6)))
+        move(v("TW", tw + DS, tw + HS, 3), v("WT", wt, wt + K))
+        ts(L(0, 16), S(64, 16), float(HS), Op.add)
+        if r < R - 1:
+            move(v("TW", tn, tn + 256), ind(v("TW", tw, tw + WN), L(0, 16)))
+        else:
+            line(v("TO", 0, 256), ind(v("TW", tw, tw + WN), L(0, 16)), 1.0, -1.0)
+    kin[0] = 10
+    eq, es = v("FQ", 256 * R, 256 * R + 256), v("FS", 256 * R, 256 * R + 256)
+    quant(eq, es, v("WB" if R % 2 else "WA", 0, 1024))
+    mm(v("P5", 0, 256), [(v("VQ", 0, 128), v("VS", 0, 128), eq, es)])
+    move(v("YS", 0, 256), v("P5", 0, 256))
+    dma("s", lambda: T.oc[:], lambda: u8(eq), [eq], [], 2200, "st")
+    for k in range(4):
+        dma("sa"[k % 2], lambda k=k: T.osc[4 * k:4 * k + 4, 0:256], lambda k=k: T.FS[32 * k:32 * k + 4, 256 * R:256 * R + 256],
+            [es], [], 2000, "st")
+    dma("s", lambda: T.y[:], lambda: T.YS[:], [v("YS", 0, 256)], [], 2200, "st")
+    dma("s", lambda: T.om[:], lambda: T.TO[0:128:16, 0:256], [v("TO", 0, 256)], [], 2000, "st")
+    return ops, sum(sends)
+
+
+def rank_program(g, core, T, topo):
+    cores = list(T.cores)
+    n = len(cores)
+    rank = T.rank_of(core)
+    if rank is None:
+        for i in range(n):
+            a, b = cores[i], cores[(i + 1) % n]
+            if _relay(topo, cores, a, b) != core:
+                continue
+            rid, pid = topo.addr(b, core)
+            i0, i1 = _halves(topo, a, core)
+            e0, e1 = _halves(topo, core, b)
+            for r in range(R):
+                lo = 160 * r + 128
+                g.wait_ge(T.sem["ac%d" % r], len(i0))
+                g.remote_dma(T.LC[:, lo:lo + 32].bitcast(dt.uint8), T.RC[:, 32 * r:32 * r + 32].bitcast(dt.uint8),
+                             T.sem["ac%d" % r], T.sem.sent, pid, rid, _mask(e0))
+                g.wait_ge(T.sem["as%d" % r], len(i1))
+                g.remote_dma(T.LS[:, lo:lo + 32], T.RS[:, 32 * r:32 * r + 32],
+                             T.sem["as%d" % r], T.sem.sent, pid, rid, _mask(e1))
+            g.wait_ge(T.sem.sent, R * (len(e0) + len(e1)))
+        return
+    nxt, prv = cores[(rank + 1) % n], cores[(rank - 1) % n]
+    via = _relay(topo, cores, core, nxt)
+    frm = _relay(topo, cores, prv, core)
+    i0, i1 = _halves(topo, prv if frm is None else frm, core)
+    ops, sent = _calls(g, T, nxt if via is None else via, topo, core, via is None)
+    deps, (_, order, way, at) = _plan(ops)
+    queue = {"v": g.vector, "a": g.scalar, "t": g.tensor, "g": g, "s": g.sync}
+    count = {"v": 0, "a": 0, "t": 0, "g": 0, "st": 0}
+    known = {q: {} for q in queue}
+    for i in order:
+        o = ops[i]
+        q, _, emit = o["ways"][way[i]]
+        if o["kind"] == "n":
+            o["done"] = {"ac%d" % o["round"]: len(i0), "as%d" % o["round"]: len(i1)}
+            o["knew"] = {}
+            continue
+        kn, need = known[q], {}
+        for j in deps[i]:
+            for s, c in ops[j]["done"].items():
+                if kn.get(s, 0) < c and need.get(s, (0, 0))[0] < c:
+                    need[s] = (c, j)
+        for s in sorted(need, key=lambda s: -at[need[s][1]]):
+            c, j = need[s]
+            if kn.get(s, 0) >= c:
+                continue
+            queue[q].wait_ge(T.sem[s], c)
+            kn[s] = c
+            for s2, c2 in ops[j]["knew"].items():
+                kn[s2] = max(kn.get(s2, 0), c2)
+        o["knew"] = dict(kn)
+        ins = emit()
+        if o["kind"] == "r":
+            o["done"] = {}
+        elif o["kind"] == "d":
+            ins.then_inc(T.sem[o["sem"]], 16)
+            count[o["sem"]] = count.get(o["sem"], 0) + 16
+            o["done"] = {o["sem"]: count[o["sem"]]}
+        else:
+            count[q] += 1
+            ins.then_inc(T.sem[q], 1)
+            o["done"] = {q: count[q]}
+    for s in count:
+        g.wait_ge(T.sem[s], count[s])
+    g.wait_ge(T.sem.sent, sent)

@@ -1,17 +1,22 @@
+import math
+from concourse.bass import DstId, RemoteDMATransfer
 from concourse.mybir import dt, AluOpType, AxisListType, ActivationFunctionType
 
 R, P, K, A = 3, 256, 32, 96
-ROWS = [[9, 10], [9, 10], [9, 10]]
-AM = 14
-SEED, SLACK, SAME, CROSS, RING = 1, 0, 60, 100, 6000.0
-URGE = [-42e3, -42e3, 137e3, 142e3, -38e3, 37e3, 371e3, -179e3, 128e3, 500.0, 5500.0, -256e3, -52e3, -163e3]
-TRIES, LEAN = 2500, 0.6
-DS, HS = 256, 352
+ROWS = [[9, 7], [9, 7], [9, 7]]
+AM = 12
+SAME, CROSS, RING, PERIOD = 60, 100, 5000.0, 19000.0
+DUE = {"setup": 9e4, "start": 0, "lay0": 1300, "rows0": 5800, "send": 7800, "lay1": 4500, "source": 12000,
+       "rows1": 12700, "writers": 14200, "keepers": 14000, "count": 16000, "free": 19000, "layer": 19000, "copy": 23000}
+SEED, TRIES, WARM, MIX = 1, 900000, 80.0, 0.5
+DS, HS = 256, 384
 WN = HS + A
 BIG = 1e29
 HOLD = 1024.0
 BF, F16, F32, I32, U16, CODE, U8 = "bfloat16", "float16", "float32", "int32", "uint16", "float8_e4m3fn_x4", "uint8"
-FLW, SCW = 256 * (AM + 1), 128 * (AM + 1) + 16
+FLW, SCW = 256 * AM, 128 * AM + 16
+CW, SW, PW = K + P, 128 + P, A + 1024
+TWN = 4 * WN
 
 
 def _sb(n, d):
@@ -22,25 +27,25 @@ SCRATCH = {
     "M0": _sb(1024, BF), "UT": _sb(512, BF), "VT": _sb(512, BF), "PT": _sb(16, I32),
     "WC": _sb(512, CODE), "WS": _sb(512, U8), "UQ": _sb(128, CODE), "US": _sb(128, U8),
     "UP": _sb(256, CODE), "UPS": _sb(256, U8), "VQ": _sb(128, CODE), "VS": _sb(128, U8),
-    "ET": _sb(2048, BF), "EQ": _sb(512, CODE), "ES": _sb(512, U8), "ZERO": _sb(896, BF),
-    "WA": _sb(4 * WN, BF), "WB": _sb(4 * WN, BF), "FQ": _sb(256 * 4, CODE), "FS": _sb(256 * 4, U8),
+    "ET": _sb(2048, BF), "EQ": _sb(512, CODE), "ES": _sb(512, U8), "ZERO": _sb(1024, BF),
+    "WA": _sb(4 * WN, BF), "WB": _sb(4 * WN, BF), "FQ": _sb(CW * 4, CODE), "FS": _sb(SW * 4, U8),
     "BT": _sb(512, BF), "BQ": _sb(128 * R, CODE), "BS": _sb(128 * R, U8),
-    "LC": _sb(608, CODE), "LS": _sb(608, U8), "RC": _sb(32 * R, CODE), "RS": _sb(32 * R, U8),
+    "RC": _sb(32 * R, CODE), "RS": _sb(128 * R, U8),
     "ZT": _sb(512, BF), "ZQ": _sb(128, CODE), "ZS": _sb(128, U8), "RB": _sb(4 * A, F32),
-    "IOF": _sb(HS, F32), "IOB": _sb(256, BF), "IOP": _sb(256, BF), "N16": _sb(256, F32), "CI": _sb(24, I32),
-    "CF": _sb(176, F32), "UL": _sb(16, U16), "MK": _sb(256, F32), "DM": _sb(256, F32),
-    "KH": _sb(256, F32), "KX": _sb(384, BF),
+    "IOF": _sb(256, F32), "IOB": _sb(HS, BF), "IOP": _sb(256, BF), "N16": _sb(256, BF), "CI": _sb(24, I32),
+    "CF": _sb(64, F32), "UL": _sb(16, U16), "MK": _sb(256, BF), "DM": _sb(256, F32),
+    "KH": _sb(256, F32), "KX": _sb(400, BF), "K4": _sb(4 * A, BF), "DK": _sb(256 * 4, BF),
+    "G16": _sb(3 * 272, BF), "HU": _sb(2 * 272, BF), "HW": _sb(6 * 256, BF),
     "ZZ": _sb(1024, F32), "TA": _sb(512, F32), "D1": _sb(512, F32), "HF": _sb(512, F32),
-    "FL": _sb(2 * FLW, F16), "SC": _sb(2 * SCW, F16), "SG": _sb(2 * 4096, BF),
-    "RI": _sb(32 * R, I32), "SM": _sb(512 * R, F32), "LI": _sb(192 * R + 64, U16),
-    "OF": _sb(256, BF), "OM": _sb(128, F16), "S1": _sb(256, F32), "ZF": _sb(256, F32), "ZM": _sb(A, F32),
-    "TW": _sb(2 * WN, BF), "WT": _sb(768 * R, BF), "TL": _sb(128, BF), "HJ": _sb(17 * 128, BF),
-    "TB": _sb(3 * A, BF), "TF": _sb(4 * A, F32), "TO": _sb(256, F32), "YS": _sb(256, F32),
-    "P0": ("psum", [128, 512], F32), "P1": ("psum", [128, 512], F32), "P2": ("psum", [128, 512], F32),
-    "P3": ("psum", [128, 512], F32), "P4": ("psum", [128, 512], F32), "P5": ("psum", [128, 512], F32),
+    "FL": _sb(2 * FLW, F16), "SC": _sb(2 * SCW, F16), "SG": _sb(2 * 4096, BF), "FD": _sb(1024, F16),
+    "RI": _sb(64 * R, I32), "SM": _sb(512 * R, F32), "LI": _sb(208 * R + 80, U16),
+    "OF": _sb(256, BF), "OM": _sb(160, F16), "S1": _sb(256, BF), "ZF": _sb(256, BF), "ZM": _sb(2 * A, F16),
+    "TW": _sb(2 * TWN, BF), "WT": _sb(PW * R, BF), "TL": _sb(128, BF), "TM": _sb(128, F16), "HJ": _sb(7 * 128, BF),
+    "TB": _sb(224, BF), "TF": _sb(3 * A, F16), "TO": _sb(256, F32), "YS": _sb(256, F32),
 }
-SEMAPHORES = (["v", "a", "t", "g", "st", "sent"] + ["d%d" % i for i in range(16)]
-              + ["ac%d" % r for r in range(R)] + ["as%d" % r for r in range(R)])
+for _i in range(8):
+    SCRATCH["P%d" % _i] = ("psum", [128, 512], F32)
+SEMAPHORES = ["v", "a", "t", "g", "st", "sent"] + ["d%d" % i for i in range(32)] + ["ac%d" % r for r in range(R)]
 PLAN = {}
 
 
@@ -51,18 +56,21 @@ def _mask(es):
     return m
 
 
-def _halves(topo, a, b):
-    es = topo.engines(a, b)
-    h = len(es) // 2
-    return es[:h], es[h:]
-
-
 def _relay(topo, cores, a, b):
     if topo.may_write(a, b):
-        return None
+        return [b, b]
     c = [x for x in topo.cores_of(a) if x not in cores and topo.may_write(x, b)]
     c.sort(key=lambda x: topo.die(x) != topo.die(a))
-    return c[0]
+    return c[:2]
+
+
+def _hop(g, T, topo, core, to, r, codes, scales):
+    es = topo.engines(core, to[0])
+    h = len(es) // 2
+    return g.remote_dma_fused(
+        [RemoteDMATransfer(dst_ids=[DstId(rid=topo.addr(b, core)[0], pnc=topo.addr(b, core)[1])], src=x, dst=o,
+                           dma_engine_mask=_mask(e), remote_sem=T.sem["ac%d" % r])
+         for b, e, (o, x) in zip(to, (es[:h], es[h:]), (codes, scales))], local_sem=T.sem.sent)
 
 
 def _overlap(x, y):
@@ -74,12 +82,14 @@ def _overlap(x, y):
 
 
 def _deps(ops):
-    out = []
+    out, above = [], []
     for i, o in enumerate(ops):
-        d = set(o["after"])
-        for j in range(i):
+        d, seen = [], 0
+        for j in range(i - 1, -1, -1):
+            if seen >> j & 1:
+                continue
             p = ops[j]
-            hit = False
+            hit = j in o["after"]
             for w in p["w"]:
                 if any(_overlap(w, x) for x in o["r"]) or any(_overlap(w, x) for x in o["w"]):
                     hit = True
@@ -90,85 +100,87 @@ def _deps(ops):
                         (len(p["ways"]) > 1 or len(o["ways"]) > 1 or p["ways"][0][0] != o["ways"][0][0]):
                     hit = True
             if hit:
-                d.add(j)
+                d.append(j)
+                seen |= above[j] | 1 << j
         out.append(d)
+        above.append(seen if o["kind"] in "cd" else 0)
     return out
 
 
-def _schedule(ops, deps, succ, bonus, lean, slack):
-    n = len(ops)
-    pr = [0.0] * n
-    for i in range(n - 1, -1, -1):
-        pr[i] = ops[i]["least"] + max([pr[j] + 80 for j in succ[i]] + [0.0])
-    pr = [p + b for p, b in zip(pr, bonus)]
-    left = [len(d) for d in deps]
-    free, end, at, way, order, on = {}, [0.0] * n, [0.0] * n, [0] * n, [], [""] * n
-    ready = {i: [0.0] * len(ops[i]["ways"]) for i in range(n) if not left[i]}
-    while ready:
-        cand = []
-        for i, t in ready.items():
-            pick = None
-            for k, w in enumerate(ops[i]["ways"]):
-                s = max(free.get(w[0], 0.0), t[k])
-                e = s + w[1] + (lean[i] if k == 0 else 0.0)
-                if pick is None or e < pick[0]:
-                    pick = (e, s, k, w[0])
-            cand.append((pick[1], i, pick[2], pick[3]))
-        first = min(cand)
-        s, i, k, _ = max([c for c in cand if c[3] == first[3] and c[0] <= first[0] + slack], key=lambda c: pr[c[1]])
-        del ready[i]
-        w = ops[i]["ways"][k]
-        free[w[0]] = s + w[1]
-        end[i], at[i], way[i], on[i] = s + w[1] + ops[i]["lat"], s, k, w[0]
-        order.append(i)
-        for j in succ[i]:
-            left[j] -= 1
-            if not left[j]:
-                ready[j] = [max(end[d] + (SAME if on[d] == u[0] else CROSS) for d in deps[j]) for u in ops[j]["ways"]]
-    return max(end), order, way, at
-
-
 def _plan(ops):
-    if "p" not in PLAN:
-        deps = _deps(ops)
-        n = len(ops)
-        succ = [[] for _ in ops]
-        for i in range(n):
-            ops[i]["least"] = min(w[1] for w in ops[i]["ways"]) + ops[i]["lat"]
-            for j in deps[i]:
-                succ[j].append(i)
-        both = [i for i in range(n) if len(ops[i]["ways"]) > 1]
-        bonus, lean, slack = [URGE[o["kin"]] for o in ops], [LEAN * o["ways"][0][1] for o in ops], SLACK
-        best = _schedule(ops, deps, succ, bonus, lean, slack)
-        now = best[0]
-        x = [SEED]
+    if "p" in PLAN:
+        return PLAN["p"]
+    deps = _deps(ops)
+    n = len(ops)
+    succ = [[] for _ in ops]
+    late = [o["due"] for o in ops]
+    for i in range(n - 1, -1, -1):
+        late[i] -= ops[i]["ways"][-1][1] + ops[i]["lat"]
+        for j in deps[i]:
+            succ[j].append(i)
+            late[j] = min(late[j], late[i] - 1.0)
+    ways = [[("vatgsn".index(w[0]), w[1]) for w in o["ways"]] for o in ops]
+    lat = [o["lat"] for o in ops]
 
-        def draw(m):
-            x[0] = (x[0] * 1103515245 + 12345) % 2147483648
-            return (x[0] >> 8) % m
+    def times(order, way, lo, hi, at, end, on, free):
+        for i in order[lo:hi]:
+            q, c = ways[i][way[i]]
+            t = free[q]
+            for d in deps[i]:
+                e = end[d] + (SAME if on[d] == q else CROSS)
+                if e > t:
+                    t = e
+            at[i], free[q], end[i], on[i] = t, t + c, t + c + lat[i], q
 
-        for t in range(TRIES):
-            b, le, sl = list(bonus), list(lean), slack
-            for _ in range(draw(4)):
-                i, d = draw(n), draw(12001) - 6000.0
-                for j in range(i, min(n, i + 1 + draw(10))):
-                    b[j] += d
-            if draw(3) == 0:
-                k, d, lo = draw(len(URGE)), draw(12001) - 6000.0, draw(3 * n) - 2 * n
-                hi = lo + n // 3 if lo > 0 else n
-                for j in range(max(lo, 0), min(hi, n)):
-                    if ops[j]["kin"] == k:
-                        b[j] += d
-            for _ in range(draw(3)):
-                le[both[draw(len(both))]] = (-3000.0, 0.0, 300.0, 3000.0)[draw(4)]
-            if draw(12) == 0:
-                sl = 40 * draw(8)
-            s = _schedule(ops, deps, succ, b, le, sl)
-            if s[0] <= now + 150.0 * (1.0 - t / TRIES):
-                now, bonus, lean, slack = s[0], b, le, sl
-                if s[0] < best[0]:
-                    best = s
-        PLAN["p"] = (deps, best)
+    x = [SEED]
+
+    def draw(k):
+        x[0] = (x[0] * 1103515245 + 12345) % 2147483648
+        return (x[0] >> 8) % k
+
+    order, way = sorted(range(n), key=lambda i: late[i]), [len(w) - 1 for w in ways]
+    at, end, on = [0.0] * n, [0.0] * n, [0] * n
+    best = (1e9,)
+    for t in range(TRIES):
+        if t % 200 == 0:
+            times(order, way, 0, n, at, end, on, [0.0] * 6)
+            order = sorted(order, key=lambda i: (at[i], i))
+            now = max(end) + MIX * sum(at) / n
+            if max(end) < best[0]:
+                best = (max(end), order, way, list(at))
+        p = k = draw(n)
+        i, o2, w2 = order[p], order, way
+        flip = len(ways[i]) > 1 and draw(10) < 3
+        if flip:
+            w2 = list(way)
+            w2[i] = 1 - w2[i]
+        if not flip or draw(2):
+            far = 1 + draw((2, 8, 20, 60)[draw(4)])
+            o2 = order[:p] + order[p + 1:]
+            if draw(2):
+                while k > max(0, p - far) and o2[k - 1] not in deps[i]:
+                    k -= 1
+            else:
+                while k < min(n - 1, p + far) and o2[k] not in succ[i]:
+                    k += 1
+            if k == p and not flip:
+                continue
+            o2.insert(k, i)
+        room = -(WARM * (1.0 - t / TRIES) + 1.0) * math.log((1.0 + draw(65536)) / 65536.0)
+        a2, e2, n2, free = list(at), list(end), list(on), [0.0] * 6
+        lo, hi = min(p, k), max(p, k) + 50
+        for j in order[max(0, lo - 30):lo] if ways[i][0][0] < 2 else order[:lo]:
+            free[on[j]] = end[j] - lat[j]
+        times(o2, w2, lo, hi, a2, e2, n2, free)
+        moved = [a2[j] - at[j] for j in o2[hi - 25:hi]]
+        if moved and min(moved) > room:
+            continue
+        if any(moved):
+            times(o2, w2, hi, n, a2, e2, n2, free)
+        new = max(e2) + MIX * sum(a2) / n
+        if new - now <= room:
+            now, order, way, at, end, on = new, o2, w2, a2, e2, n2
+    PLAN["p"] = (deps, best)
     return PLAN["p"]
 
 
@@ -176,7 +188,7 @@ def _calls(g, T, to, topo, core, land):
     Op, Fn = AluOpType, ActivationFunctionType
     ops = []
     nd = [0]
-    kin = [0]
+    due = [0.0, "setup"]
 
     def v(name, lo, hi, st=1):
         return (name, lo, hi, st)
@@ -187,6 +199,9 @@ def _calls(g, T, to, topo, core, land):
         if isinstance(x, tuple):
             return T[x[0]][:, x[1]:x[2]:x[3]] if x[3] > 1 else T[x[0]][:, x[1]:x[2]]
         return x
+
+    def group(x, k=0):
+        return T[x[0]][16 * k:16 * k + 16, x[1]:x[2]]
 
     def ind(w, o):
         return ("ind", w, o)
@@ -206,7 +221,7 @@ def _calls(g, T, to, topo, core, land):
 
     def add(q, cost, r, w, emit, lat=0.0, kind="c", after=()):
         ops.append({"ways": [(q, cost, emit)], "lat": lat, "r": r, "w": w, "kind": kind, "after": list(after),
-                    "kin": kin[0]})
+                    "kin": due[1], "due": due[0] + DUE[due[1]]})
         return len(ops) - 1
 
     def either():
@@ -234,12 +249,12 @@ def _calls(g, T, to, topo, core, land):
         else:
             add("v", 55 + size(o) * rate(o, x), regs(x), [o], lambda: g.vector.tensor_copy(ap(o), ap(x)))
 
-    def scan(o, d0, d1, op0, op1):
+    def scan(o, d0, d1, op0, op1, first=0.0):
         add("v", 55 + size(o) * (0.5 if two(o, d0, d1) else 1.0), [d0, d1], [o],
-            lambda: g.vector.tensor_tensor_scan(ap(o), ap(d0), ap(d1), 0.0, op0, op1))
+            lambda: g.vector.tensor_tensor_scan(ap(o), ap(d0), ap(d1), first, op0, op1))
 
-    def hold(o, x):
-        scan(o, v("KX", 0, size(x)), x, Op.add, Op.max)
+    def hold(o, x, k="KX"):
+        scan(o, v(k, 0, size(x)), x, Op.add, Op.max)
 
     def fill(o, c):
         add("v", 55 + size(o) * (0.5 if two(o) else 1.0), [], [o], lambda: g.vector.memset(ap(o), c))
@@ -270,16 +285,17 @@ def _calls(g, T, to, topo, core, land):
         act(o, x, Fn.Relu if relu else Fn.Identity, bias=None if relu else b, scale=a)
         either()
 
+    def nil(o, x, a):
+        ts(o, x, 0.0, Op.is_equal, a, Op.mult)
+        act(o, x, Fn.Relu, bias=a, scale=-a)
+        either()
+
     def quant(c, s, x):
         add("v", 30 + size(x) * 0.27, [x], [c, s], lambda: g.vector.quantize_mx(ap(c), ap(s), ap(x)))
 
-    def mm(o, parts):
-        def e():
-            ins = None
-            for i, (a, b, c, d) in enumerate(parts):
-                ins = g.tensor.matmul_mx(ap(o), ap(a), ap(b), ap(c), ap(d), i == 0, i == len(parts) - 1)
-            return ins
-        add("t", len(parts) * (size(o) + 16) * 0.65, [x for p in parts for x in p], [v(o[0], 0, 512)], e, lat=100.0)
+    def mm(o, a, b, c, d):
+        add("t", (size(o) + 16) * 0.65, [a, b, c, d], [v(o[0], 0, 512)],
+            lambda: g.tensor.matmul_mx(ap(o), ap(a), ap(b), ap(c), ap(d), True, True), lat=100.0)
 
     def iota(o, pat, base=0, cm=0):
         def e():
@@ -288,45 +304,66 @@ def _calls(g, T, to, topo, core, land):
             return g.iota(ap(o), pat, base, cm, allow_small_or_imprecise_dtypes=True)
         add("g", 150 + 2 * size(o), [], [o], e)
 
-    def dma(q, out, in_, r, w, lat, sem=None):
+    def keep(o, x, pat, op, other, base, cm, on=ap):
+        add("g", 190 + 2 * size(o), [x], [o], lambda: g.affine_select(on(o), on(x), pat, op, other, base, cm))
+
+    def dma(q, out, in_, r, w, lat, sem=None, times=1):
         if sem is None:
             sem = "d%d" % nd[0]
             nd[0] += 1
         eng = g.sync if q == "s" else g.scalar
-        i = add(q, 80, r, w, lambda: eng.dma_start(out(), in_()), lat=lat, kind="d")
+        i = add(q, 80 * times, r, w, lambda: [eng.dma_start(out(k), in_(k)) for k in range(times)], lat=lat, kind="d")
         ops[i]["sem"] = sem
+
+    def copy(o, x):
+        dma("s", lambda k: ap(o), lambda k: ap(x), [x] + m0, [o], 2500)
 
     def u8(x):
         return ap(x).bitcast(dt.uint8)
 
-    dma("s", lambda: T.M0[:], lambda: T.m[:], [], [v("M0", 0, 1024)], 2600)
-    dma("a", lambda: T.PT[:], lambda: T.pt[:], [], [v("PT", 0, 16)], 2000)
-    dma("a", lambda: T.UT[:], lambda: T.u[:], [], [v("UT", 0, 512)], 2400)
-    dma("s", lambda: T.WC[:].bitcast(dt.uint8), lambda: T.wc[:], [], [v("WC", 0, 512)], 3000)
-    dma("s", lambda: T.WS[:], lambda: T.ws[:], [], [v("WS", 0, 512)], 3000)
-    dma("s", lambda: T.VT[:], lambda: T.v[:], [], [v("VT", 0, 512)], 3000)
-    fill(v("ZERO", 0, 896), 0.0)
-    for x in [v("TW", 0, 2 * WN), v("BT", 128, 512), v("ZT", 4 * A, 512), v("WA", 1024, 4 * WN), v("WB", 1024, 4 * WN)] + \
-            [v("WT", 768 * r, 768 * r + 768) for r in range(R)]:
-        z = v("ZERO", 0, size(x))
-        dma("s", lambda x=x: ap(x), lambda z=z: ap(z), [z], [x], 2500)
+    def fq(r, lo=K, n=P):
+        return v("FQ", CW * r + lo, CW * r + lo + n), v("FS", SW * r + 128 - K + lo, SW * r + 128 - K + lo + n)
+
+    dma("s", lambda k: T.M0[:], lambda k: T.m[:], [], [v("M0", 0, 1024)], 2600)
+    dma("a", lambda k: T.PT[:], lambda k: T.pt[:], [], [v("PT", 0, 16)], 2000)
+    dma("a", lambda k: T.UT[:], lambda k: T.u[:], [], [v("UT", 0, 512)], 2400)
+    m0 = [v("M0", 0, 1024)]
+    dma("s", lambda k: T.WC[:].bitcast(dt.uint8), lambda k: T.wc[:], m0, [v("WC", 0, 512)], 3000)
+    dma("s", lambda k: T.WS[:], lambda k: T.ws[:], m0, [v("WS", 0, 512)], 3000)
+    dma("s", lambda k: T.VT[:], lambda k: T.v[:], m0, [v("VT", 0, 512)], 3000)
+    fill(v("ZERO", 0, 1024), 0.0)
+    for x in [v("TW", TWN // 2 * h, TWN // 2 * (h + 1)) for h in range(4)] + \
+            [v("BT", 0, 384), v("ZT", 4 * A, 512), v("WA", 4 * DS, 4 * HS), v("WB", 4 * DS, 4 * HS)] + \
+            [v("WT", PW * r + A + 256, PW * r + A + 512) for r in range(R)]:
+        copy(x, v("ZERO", 0, size(x)))
     iota(v("CI", 0, 1), [[0, 1]], 0, 1)
     iota(v("N16", 0, 256), [[0, 16], [1, 16]])
     iota(v("CI", 8, 24), [[1, 2], [16, 8]])
-    iota(v("IOF", 0, HS), [[1, HS]])
-    iota(v("IOB", 0, 256), [[1, 256]])
+    iota(v("IOF", 0, 256), [[1, 256]])
+    iota(v("IOB", 0, HS), [[1, HS]])
     iota(v("IOP", 0, 256), [[1, 16], [16, 16]], 1)
+    iota(v("K4", A, 2 * A), [[0, A // 4], [1, 4]])
     for h in range(4):
-        x = v("ET", 512 * h, 512 * h + 512)
-        iota(x, [[0, 512]], 1)
-        add("g", 170 + 1024, [x], [x], lambda x=x, h=h: g.affine_select(
-            ap(x), ap(x), [[-4, 128], [-1, 4]], Op.is_equal, 0.0, h, 4))
+        keep(v("ET", 512 * h, 512 * h + 512), v("ZERO", 0, 512), [[-4, 128], [-1, 4]], Op.not_equal, 1.0, h, 4)
+    dk = {}
+    for a in sorted(set(sum(ROWS, []))):
+        b = dk[a] = 256 * len(dk)
+        iota(v("DK", b, b + 16 * (16 - a)), [[0, 16 - a], [1024, 16]])
+        iota(v("DK", b + 16 * (16 - a), b + 256), [[0, a], [1024, 16]], -128)
+    for d in range(3):
+        keep(v("G16", 0, 272), v("G16" if d else "ZERO", 0, 272), [[-1, 272]], Op.not_equal, 256.0 ** d, 15 + d, 16, group)
+    iota(v("G16", 544, 816), [[0, 16], [1, 17]])
+    keep(v("G16", 272, 544), v("G16", 544, 816), [[-1, 16], [0, 17]], Op.is_gt, 0.0, 0, 1, group)
+    dma("s", lambda k: group(v("HU", 0, 544), k), lambda k: group(v("G16", 0, 544)), [v("G16", 0, 544)],
+        [v("HU", 0, 544)], 2500, times=8)
+    for b in range(6):
+        copy(v("HW", 256 * b, 256 * b + 256), v("HU", 15 - 3 * b, 271 - 3 * b))
     ts(v("CI", 1, 2), v("CI", 0, 1), 15, Op.bitwise_and)
-    ts(v("CI", 2, 3), v("CI", 0, 1), 31, Op.bitwise_and)
-    cp(v("CF", 0, 2), v("CI", 1, 3))
-    q, p32, q16, top, q1, hq = [v("CF", i, i + 1) for i in range(6)]
-    JW, THR, C256, M32 = v("CF", 8, 24), 24, v("CF", 48, 64), v("CF", 64, 96)
-    HT, h256, h255, h31 = 160, v("CF", 164, 165), v("CF", 165, 166), v("CF", 166, 167)
+    ts(v("CI", 2, 3), v("CI", 0, 1), 2, Op.arith_shift_right, 3, Op.bitwise_and)
+    ts(v("CI", 3, 4), v("CI", 0, 1), 3, Op.bitwise_and)
+    cp(v("CF", 0, 3), v("CI", 1, 4))
+    q, qh, ql, hq, hq4, qh1, h4, hb, hm, h127, q16, q17 = [v("CF", i, i + 1) for i in range(12)]
+    JW, PC, KC = v("CF", 16, 32), v("CF", 32, 48), v("CF", 48, 54)
     cp(v("UL", 0, 16), v("CI", 8, 24))
     ts(v("MK", 0, 256), v("N16", 0, 256), q, Op.is_equal)
     line(v("DM", 0, 256), v("MK", 0, 256), -2 * BIG, BIG)
@@ -334,26 +371,26 @@ def _calls(g, T, to, topo, core, land):
     fill(v("KH", 0, 256, 16), 3 * BIG)
     for o in range(2):
         cp(v("SC", SCW * o, SCW * o + 1), v("ZERO", 0, 1))
-    line(q1, q, 1.0, 1.0)
+    fill(v("TB", 0, 1), 0.0)
     ts(hq, q, 15.0, Op.is_lt, -HOLD, Op.mult)
-    ts(v("KX", 128, 256), v("N16", 0, 128), q1, Op.is_equal, HOLD, Op.mult)
-    line(v("KX", 256, 384), v("MK", 0, 128), -4 * HOLD, 0.0)
-    tt(v("KX", 0, 128), v("KX", 128, 256), v("KX", 256, 384), Op.add)
-    line(v("CF", 7, 8), hq, 4.0, 0.0)
-    line(v("CF", HT, HT + 4), v("IOF", 0, 4), 1.0, v("CF", 7, 8))
-    line(h256, hq, -1.0, 256.0)
-    line(h255, hq, 1.0, 255.0)
-    line(h31, hq, 1.0, 31.0)
-    line(q16, q, -16.0, -0.5)
-    ts(top, p32, q, Op.subtract, 15.0, Op.add)
+    line(hq4, hq, 4.0, 0.0)
+    fill(v("KX", 128, 129), 0.0)
+    line(v("KX", 129, 257), v("MK", 0, 128), HOLD, 0.0)
+    line(v("KX", 272, 400), v("MK", 0, 128), -4 * HOLD, 0.0)
+    tt(v("KX", 0, 128), v("KX", 128, 256), v("KX", 272, 400), Op.add)
+    line(qh1, qh, 1.0, 1.0)
+    ts(h4, qh, 3.0, Op.is_lt, -4 * HOLD, Op.mult)
+    line(hb, h4, 1.0, ql)
+    ts(v("K4", 2 * A, 3 * A), v("K4", A, 2 * A), qh1, Op.is_equal, HOLD, Op.mult)
+    ts(v("K4", 3 * A, 4 * A), v("K4", A, 2 * A), qh, Op.is_equal, -4 * HOLD, Op.mult)
+    tt(v("K4", 0, A), v("K4", 2 * A, 3 * A), v("K4", 3 * A, 4 * A), Op.add)
+    line(hm, hq, 1.0, -1.0)
+    line(h127, hq, 1.0, 127.0)
+    line(q16, q, 16.0, -255.0)
+    line(q17, q, 17.0, 0.0)
     ts(JW, v("IOF", 0, 256, 16), q, Op.add, -float(HS), Op.add)
-    line(v("CF", THR, THR + 17), v("IOF", 0, 17), -1.0, q16)
-    line(C256, v("CF", THR, THR + 16), -1.0, 255.5)
-    ts(v("CF", 96, 128), v("IOF", 0, 32), p32, Op.is_gt)
-    ts(v("CF", 128, 160), v("IOF", 0, 32), top, Op.is_le)
-    tt(M32, v("CF", 96, 128), v("CF", 128, 160), Op.mult)
-    for r in range(R + 1):
-        quant(v("LC", 160 * r, 160 * r + 128), v("LS", 160 * r, 160 * r + 128), v("ZERO", 0, 512))
+    line(PC, v("IOF", 0, 16), 1.0, q16)
+    ts(KC, v("IOF", 0, A, 16), q, Op.add, h127, Op.subtract)
     quant(v("EQ", 0, 512), v("ES", 0, 512), v("ET", 0, 2048))
     quant(v("UQ", 0, 128), v("US", 0, 128), v("UT", 0, 512))
     ul = v("UL", 0, 16)
@@ -361,55 +398,51 @@ def _calls(g, T, to, topo, core, land):
         T.UP[:, 0:256].bitcast(dt.uint32), T.UQ[:, 0:128].bitcast(dt.uint32).indirect(ap(ul))))
     move(v("UPS", 0, 256), ind(v("US", 0, 128), ul))
     quant(v("VQ", 0, 128), v("VS", 0, 128), v("VT", 0, 512))
-    l0 = 192 * R
+    l0 = 208 * R
     for t in range(4):
         ts(v("LI", l0 + 16 * t, l0 + 16 * t + 16), v("PT", 0, 16), 4.0, Op.mult, float(t), Op.add)
         move(v("WA", t, 1024, 4), ind(v("M0", 0, 1024), v("LI", l0 + 16 * t, l0 + 16 * t + 16)))
-    p16 = v("LI", 192 * (R - 1) + 176, 192 * R)
-    kin[0] = 1
+    p16 = v("LI", l0 + 64, l0 + 80)
     cp(p16, v("PT", 0, 16))
-    line(v("TW", 0, 256), ind(v("IOF", 0, 256), p16), 1.0, 1.0)
+    line(v("TW", 0, 1024, 4), ind(v("IOF", 0, 256), p16), 1.0, 1.0)
 
     def ranks(r, o, out):
         a = ROWS[r][o]
-        kin[0] = 4 + 3 * o
+        n = 16 - a
+        due[1] = "lay%d" % o
         pv, pa = v("P%d" % (2 * o), 0, 256), v("P%d" % (2 * o + 1), 0, 256)
-        side = (v("UP", 128 * o, 128 * o + 128), v("UPS", 128 * o, 128 * o + 128),
-                v("FQ", 256 * r, 256 * r + 256), v("FS", 256 * r, 256 * r + 256))
-        mm(pa, [side])
-        mm(pv, [side])
-        z, b, fl, sc = 512 * o, 256 * o, FLW * o, SCW * o
+        side = (v("UP", 128 * o, 128 * o + 128), v("UPS", 128 * o, 128 * o + 128)) + fq(r)
+        mm(pa, *side)
+        mm(pv, *side)
+        z, b, fl, sc, fd = 512 * o, 256 * o, FLW * o, SCW * o, 512 * o
         hf = v("HF", b, b + 256)
         act(v("TA", b, b + 256), pa, Fn.Abs, bias=2.0 ** -125, scale=1.0625 * 2.0 ** -24)
         act(v("ZZ", z + 16, z + 256), v(pa[0], 16, 256), Fn.Copy)
         tt(v("D1", b, b + 256), pv, v("DM", 0, 256), Op.max)
         scan(hf, v("KH", 0, 256), v("D1", b, b + 256), Op.add, Op.min)
         tt(v("ZZ", z + 256, z + 512), pv, v("TA", b, b + 256), Op.add)
-        tt(v("FL", fl, fl + 256), pv, hf, Op.is_equal)
+        due[1] = "rows%d" % o
+        tt(v("FD", fd, fd + 256), pv, hf, Op.is_equal)
+        scan(v("FD", fd + 256, fd + 512), v("DK", dk[a], dk[a] + 256), v("FD", fd, fd + 256), Op.min, Op.add)
         acc = 512 * r + 16 * o
-        kin[0] += 1
         for c in range(16):
             win, s = v("ZZ", z + 16 * c + 16, z + 16 * c + 272), v("HF", b + 16 * c + 15, b + 16 * c + 16)
-            if c < a:
-                ts(v("FL", fl + 256 * (c + 1), fl + 256 * (c + 2)), win, s, Op.is_gt, -0.5, Op.add)
+            if c >= n:
+                ts(v("FL", fl + 256 * (c - n), fl + 256 * (c - n + 1)), win, s, Op.is_gt, -0.5, Op.add)
             else:
                 sg = v("SG", 4096 * o + 256 * c, 4096 * o + 256 * c + 256)
                 act(sg, win, Fn.Sign, bias=s, scale=-1.0)
                 act(sg, sg, Fn.Relu, scale=-1.0, acc=v("SM", acc + c, acc + c + 1))
-        w = 128 * (a + 1)
-        kin[0] += 1
+        w = 128 * a
+        due[1] = ("send", "writers")[o]
         scan(v("SC", sc + 1, sc + 1 + w), v("FL", fl, fl + 2 * w, 2), v("FL", fl + 1, fl + 2 * w, 2), Op.add, Op.add)
-        d1, d2 = v("SM", 512 * r + 400 + 32 * o, 512 * r + 416 + 32 * o), v("SM", 512 * r + 416 + 32 * o, 512 * r + 416 + 32 * o + a)
-        tt(d1, v("SC", sc + 8, sc + 129, 8), v("SC", sc, sc + 121, 8), Op.subtract)
-        tt(d2, v("SC", sc + 256, sc + w + 1, 128), v("SC", sc + 128, sc + w - 127, 128), Op.subtract)
-        line(v("SM", acc, acc + a), d2, 1.0, 128.0)
-        tt(out, v("SM", acc, acc + 16), d1, Op.subtract)
+        tt(v("SM", acc + n, acc + 16), v("SC", sc + 128, sc + w + 1, 128), v("SC", sc, sc + w - 127, 128), Op.subtract)
+        tt(out, v("SM", acc, acc + 16), v("FD", fd + 256 + 15, fd + 512, 16), Op.subtract)
 
-    sends = []
     for r in range(R):
         W, Wn = ("WA", "WB") if r % 2 == 0 else ("WB", "WA")
-        tw, tn = WN * (r % 2), WN * (1 - r % 2)
-        li, sm, ri, wt = 192 * r, 512 * r + 32, 32 * r, 768 * r
+        tw, tn = TWN * (r % 2), TWN * (1 - r % 2)
+        li, sm, ri, wt = 208 * r, 512 * r + 32, 64 * r, PW * r
 
         def L(a, n):
             return v("LI", li + a, li + a + n)
@@ -417,128 +450,117 @@ def _calls(g, T, to, topo, core, land):
         def S(a, n):
             return v("SM", sm + a, sm + a + n)
 
-        kin[0] = 10
-        quant(v("FQ", 256 * r, 256 * r + 256), v("FS", 256 * r, 256 * r + 256), v(W, 0, 1024))
+        due[:] = [PERIOD * r, "start"]
+        quant(*fq(r), v(W, 0, 1024))
         rho, alp = v("RI", ri, ri + 16), S(432, 16)
         ranks(r, 0, rho)
         cp(L(0, 16), rho)
         cp(ind(v("OF", 0, 256), L(0, 16)), v("IOB", 0, 256))
-        hold(v("OM", 0, 128), v("OF", 0, 128))
-        for t in range(4):
-            ts(L(16 + 2 * t, 2), v("OM", 15, 32, 16), 4.0, Op.mult, v("CF", HT + t, HT + t + 1), Op.add)
-            move(v("BT", t, 128, 4), ind(v(W, 0, 1024), L(16 + 2 * t, 2)))
+        hold(v("OM", 128, 160), v("OF", 0, K), "K4")
+        ts(L(16, 8), v("OM", 131, 160, 4), 4.0, Op.mult, hb, Op.add)
+        move(v("BT", 384, 512), ind(v(W, 0, 1024), L(16, 8)))
         bq, bs = v("BQ", 128 * r, 128 * r + 128), v("BS", 128 * r, 128 * r + 128)
         quant(bq, bs, v("BT", 0, 512))
-        rid, pid = topo.addr(to, core)
-        e0, e1 = _halves(topo, core, to)
-        lc, ls = v("LC", 160 * r + 128, 160 * r + 160), v("LS", 160 * r + 128, 160 * r + 160)
-        oc_, os_ = (lc, ls) if land else (v("RC", 32 * r, 32 * r + 32), v("RS", 32 * r, 32 * r + 32))
-        bc, bp = v("BQ", 128 * r, 128 * r + 32), v("BS", 128 * r, 128 * r + 32)
-        s0 = add("g", 300, [bc], [], lambda r=r, o=oc_, x=bc, m=_mask(e0): g.remote_dma(
-            u8(o), u8(x), T.sem["ac%d" % r], T.sem.sent, pid, rid, m), kind="r")
-        s1 = add("g", 300, [bp], [], lambda r=r, o=os_, x=bp, m=_mask(e1): g.remote_dma(
-            ap(o), ap(x), T.sem["as%d" % r], T.sem.sent, pid, rid, m), kind="r", after=[s0])
-        sends.append(len(e0) + len(e1))
-        i = add("n", 0, [], [lc, ls], None, lat=RING, kind="n", after=[s0, s1])
+        lc, ls = fq(r, 0, K)[0], v("FS", SW * r, SW * r + 128)
+        oc_, os_ = (lc, ls) if land else (v("RC", K * r, K * r + K), v("RS", 128 * r, 128 * r + 128))
+        bc = v("BQ", 128 * r + 128 - K, 128 * r + 128)
+        s0 = add("g", 400, [bc, bs], [], lambda r=r, c=(oc_, bc), s=(os_, bs): _hop(
+            g, T, topo, core, to, r, (u8(c[0]), u8(c[1])), (ap(s[0]), ap(s[1]))), kind="r")
+        i = add("n", 0, [], [lc, ls], None, lat=RING, kind="n", after=[s0])
         ops[i]["round"] = r
-        kin[0] = 2
-        ts(L(24, 8), v("OM", 15, 128, 16), hq, Op.add)
-        move(v("TL", 0, 128), ind(v("TW", tw, tw + 256), L(24, 8)))
-        kin[0] = 3
+        due[1] = "keepers"
+        hold(v("OM", 0, 128), v("OF", 0, 128))
+        ts(L(24, 8), v("OM", 15, 128, 16), 4.0, Op.mult, hq4, Op.add)
+        move(v("TL", 0, 128), ind(v("TW", tw, tw + 1024), L(24, 8)))
+        hold(v("TM", 0, 128), v("TL", 0, 128))
+        ts(L(160, 8), v("TM", 15, 128, 16), hm, Op.add)
+        due[1] = "source"
         ts(v("RI", ri + 16, ri + 32), rho, 159, Op.bitwise_and)
-        ts(S(0, 16), v("RI", ri + 16, ri + 32), 3.0, Op.mult, -128.0 - HS, Op.add)
+        ts(S(0, 16), v("RI", ri + 16, ri + 32), 4.0, Op.mult, -256.0 - HS, Op.add)
         tt(S(16, 16), S(0, 16), JW, Op.max)
         ts(L(32, 16), S(16, 16), float(HS), Op.add)
-        move(v("S1", 0, 256), ind(v("IOF", 0, HS), L(32, 16)))
+        move(v("S1", 0, 256), ind(v("IOB", 0, HS), L(32, 16)))
         ranks(r, 1, alp)
         cp(L(48, 16), alp)
         cp(ind(v("ZF", 0, 256), L(48, 16)), v("S1", 0, 256))
-        hold(v("ZM", 0, A), v("ZF", 0, A))
-        zw = v("ZM", 15, A, 16)
+        hold(v("ZM", A, 2 * A), v("ZF", 0, A), "K4")
+        ts(L(64, 24), v("ZM", A + 3, 2 * A, 4), 4.0, Op.mult, hb, Op.add)
         ts(S(32, 16), alp, float(A), Op.is_ge, 1000.0, Op.mult)
         act(S(32, 16), alp, Fn.Relu, bias=-1000.0 * (A - 1), scale=1000.0)
         either()
         tt(S(48, 16), alp, S(32, 16), Op.subtract)
         tt(S(64, 16), S(48, 16), S(16, 16), Op.max)
-        kin[0] = 10
-        mm(v("P4", 0, 128), [(v("EQ", 128 * b, 128 * b + 128), v("ES", 128 * b, 128 * b + 128),
-                              v("LC", 160 * r + 128 - 32 * b, 160 * r + 256 - 32 * b),
-                              v("LS", 160 * r + 128 - 32 * b, 160 * r + 256 - 32 * b)) for b in range(4)])
+        due[1] = "layer"
         for b in range(4):
-            act(v(W, 4 * DS + b, 4 * HS, 12), v("P4", 32 * b, 32 * b + 32), Fn.Copy)
-        for t in range(4):
-            ts(L(64 + 6 * t, 6), zw, 4.0, Op.mult, v("CF", HT + t, HT + t + 1), Op.add)
-            move(v("ZT", t, 4 * A, 4), ind(v(W, 0, 4 * HS), L(64 + 6 * t, 6)))
+            mm(v("P%d" % (4 + b), 0, 128), v("EQ", 128 * b, 128 * b + 128), v("ES", 128 * b, 128 * b + 128), *fq(r, 0, 128))
+            move(v(W, 4 * DS + b, 4 * HS, 16), v("P%d" % (4 + b), 0, K))
+        for h in range(2):
+            move(v("ZT", 192 * h, 192 * h + 192), ind(v(W, 0, 4 * HS), L(64 + 12 * h, 12)))
         quant(v("ZQ", 0, 128), v("ZS", 0, 128), v("ZT", 0, 512))
         for b in range(4):
-            mm(v("P%d" % b, 0, 128), [(v("WC", 128 * b, 128 * b + 128), v("WS", 128 * b, 128 * b + 128),
-                                       v("ZQ", 0, 128), v("ZS", 0, 128))])
-            line(v("RB", A * b, A * b + A), v("P%d" % b, 0, A), 0.03125, 0.0, relu=True)
-            tt(v(W, 4 * HS + b, 4 * WN, 4), v("RB", A * b, A * b + A), v("ZT", b, 4 * A, 4), Op.add)
+            mm(v("P%d" % b, 0, 128), v("WC", 128 * b, 128 * b + 128), v("WS", 128 * b, 128 * b + 128),
+               v("ZQ", 0, 128), v("ZS", 0, 128))
+            line(v("RB", b, 4 * A, 4), v("P%d" % b, 0, A), 0.03125, 0.0, relu=True)
+        tt(v(W, 4 * HS, 4 * WN), v("RB", 0, 4 * A), v("ZT", 0, 4 * A), Op.add)
         for t in range(4):
-            ts(L(96 + 16 * t, 16), S(64, 16), 4.0, Op.mult, float(t + 4 * HS), Op.add)
-            move(v(Wn, t, 1024, 4), ind(v(W, 0, 4 * WN), L(96 + 16 * t, 16)))
-        kin[0] = 11
-        for c in range(17):
-            act(v("HJ", 128 * c, 128 * c + 128), v("TL", 0, 128), Fn.Sign, bias=v("CF", THR + c, THR + c + 1), acc=S(80 + c, 1))
-        cnt = S(112, 16)
-        kin[0] = 12
-        tt(cnt, S(80, 16), S(81, 16), Op.subtract)
+            line(S(368 + 16 * t, 16), S(64, 16), 4.0, float(t + 4 * HS))
+        cp(L(96, 64), S(368, 64))
+        parts = 2 if r == R - 1 else 1
+        for h in range(parts):
+            for t in range(4):
+                move(v(Wn, 1024 // parts * h + t, 1024 // parts * (h + 1), 4),
+                     ind(v(W, 0, 4 * WN), L(96 + 16 * t + 8 * h, 16 // parts)))
+        due[1] = "count"
+        for b in range(6):
+            act(v("HJ", 128 * b, 128 * b + 128), ind(v("HW", 256 * b, 256 * b + 256), L(160, 8)), Fn.Identity, acc=S(80 + b, 1))
+        due[1] = "free"
+        dig, cnt = v("RI", ri + 32, ri + 38), v("RI", ri + 40, ri + 56)
+        cp(dig, S(80, 6))
+        ts(v("RI", ri + 40, ri + 58, 3), dig, 255, Op.bitwise_and)
+        ts(v("RI", ri + 41, ri + 58, 3), dig, 8, Op.arith_shift_right, 255, Op.bitwise_and)
+        ts(v("RI", ri + 42, ri + 58, 3), dig, 16, Op.arith_shift_right)
         ts(S(128, 16), cnt, 0.0, Op.is_equal)
-        act(S(128, 16), cnt, Fn.Relu, bias=1.0, scale=-1.0)
-        either()
         scan(S(144, 16), v("IOF", 0, 16), S(128, 16), Op.min, Op.add)
-        ts(S(160, 32), M32, S(159, 1), Op.mult)
-        add("v", 90, [S(160, 32)], [S(192, 32)], lambda a=S(192, 32), b=S(160, 32): g.vector.transpose(ap(a), ap(b)))
-        add("v", 90, [S(192, 32)], [S(224, 1)], lambda a=S(224, 1), b=S(192, 32): g.vector.tensor_reduce(
-            ap(a), ap(b), AxisListType.X, Op.add))
-        line(S(248, 16), cnt, 1000.0, -1.0)
-        tt(S(232, 16), S(144, 16), S(248, 16), Op.add)
-        line(S(264, 16), S(232, 16), 1.0, S(224, 1))
-        act(S(280, 16), cnt, Fn.Relu, bias=512.0, scale=-128.0)
-        tt(S(296, 16), S(280, 16), C256, Op.add)
-        tt(S(312, 16), S(264, 16), S(296, 16), Op.min)
-        cp(L(160, 16), S(312, 16))
-        pages = v("WT", wt, wt + 768)
-        cp(ind(pages, L(160, 16)), v("IOP", 0, 256))
-        kin[0] = 13
-        ts(L(88, 6), zw, hq, Op.add)
-        move(v("TB", 0, A), ind(v("TW", tw, tw + HS), L(88, 6)))
-        hold(v("TF", 0, A), v("TB", 0, A))
-        at = v("TF", 15, A, 16)
-        ts(S(328, 6), zw, h256, Op.is_ge, -1000.0, Op.mult)
-        tt(S(336, 6), S(328, 6), at, Op.add)
-        ts(L(176, 6), S(336, 6), h255, Op.add, 0.0, Op.max)
-        more = v("TB", A, 2 * A)
-        ts(more, ind(pages, L(176, 6)), 0.0, Op.is_gt)
-        act(more, ind(pages, L(176, 6)), Fn.Sign)
-        either()
-        scan(v("TB", 2 * A, 3 * A), v("IOB", 0, A), more, Op.min, Op.add)
-        line(v("TF", A, 2 * A), more, -800.0, 800.0)
-        tt(v("TF", 2 * A, 3 * A), v("TF", A, 2 * A), v("TB", 2 * A, 3 * A), Op.add)
-        hold(v("TF", 3 * A, 4 * A), v("TF", 2 * A, 3 * A))
-        line(S(344, 6), at, 1.0, 480.0)
-        tt(S(352, 6), S(344, 6), v("TF", 3 * A + 15, 4 * A, 16), Op.min)
-        ts(L(182, 6), S(352, 6), h31, Op.add)
-        move(v("TW", tw + HS, tw + WN), ind(pages, L(182, 6)))
-        move(v("TW", tw + DS, tw + HS, 3), v("WT", wt, wt + K))
-        ts(L(0, 16), S(64, 16), float(HS), Op.add)
+        ts(L(192, 1), S(159, 1), q17, Op.add)
+        act(v("HJ", 768, 784), ind(v("HU", 272, 544), L(192, 1)), Fn.Identity, acc=S(224, 1))
+        ts(S(248, 16), cnt, 2.0, Op.min, 512.0, Op.mult)
+        tt(S(232, 16), S(248, 16), PC, Op.add)
+        line(S(264, 16), S(144, 16), 1.0, S(224, 1))
+        tt(S(312, 16), S(264, 16), S(232, 16), Op.max)
+        ts(L(168, 16), S(312, 16), -1.0, Op.add)
+        cp(ind(v("WT", wt + A, wt + PW), L(168, 16)), v("IOP", 0, 256))
+        due[1] = "copy"
+        move(v("TW", tw + 4 * DS, tw + 4 * HS, 16), v("WT", wt + A, wt + A + K))
+        hold(v("ZM", 0, A), v("ZF", 0, A))
+        ts(L(88, 6), v("ZM", 15, A, 16), 4.0, Op.mult, hq4, Op.add)
+        move(v("WT", wt, wt + A), ind(v("TW", tw, tw + 4 * HS), L(88, 6)))
+        hold(v("TF", 0, A), v("WT", wt, wt + A))
+        ts(L(184, 6), v("TF", 15, A, 16), hm, Op.add)
+        nil(v("TB", 1, A + 1), ind(v("WT", wt + A + 256, wt + A + 512), L(184, 6)), 128.0)
+        line(v("TB", 128, 128 + A), v("TB", 1, A + 1), 129.0 / 128.0, 0.0)
+        scan(v("TF", A, 2 * A), v("TB", 128, 128 + A), v("TB", 0, A), Op.add, Op.subtract, -128.0)
+        hold(v("TF", 2 * A, 3 * A), v("TF", A, 2 * A))
+        tt(S(352, 6), v("TF", 2 * A + 15, 3 * A, 16), KC, Op.max)
+        ts(L(194, 6), S(352, 6), h127, Op.add)
+        move(v("TW", tw + 4 * HS, tw + TWN, 4), ind(v("WT", wt, wt + A + 128), L(194, 6)))
         if r < R - 1:
-            move(v("TW", tn, tn + 256), ind(v("TW", tw, tw + WN), L(0, 16)))
+            move(v("TW", tn, tn + 1024, 4), ind(v("TW", tw, tw + TWN), L(96, 16)))
         else:
-            line(v("TO", 0, 256), ind(v("TW", tw, tw + WN), L(0, 16)), 1.0, -1.0)
-    kin[0] = 10
-    eq, es = v("FQ", 256 * R, 256 * R + 256), v("FS", 256 * R, 256 * R + 256)
-    quant(eq, es, v("WB" if R % 2 else "WA", 0, 1024))
-    mm(v("P5", 0, 256), [(v("VQ", 0, 128), v("VS", 0, 128), eq, es)])
-    move(v("YS", 0, 256), v("P5", 0, 256))
-    dma("s", lambda: T.oc[:], lambda: u8(eq), [eq], [], 2200, "st")
+            line(v("TO", 0, 256), ind(v("TW", tw, tw + TWN), L(96, 16)), 1.0, -1.0)
+    due[1] = "layer"
+    for h in range(2):
+        (eq, es), ys = fq(R, K + 128 * h, 128), v("YS", 128 * h, 128 * h + 128)
+        quant(eq, es, v("WB" if R % 2 else "WA", 512 * h, 512 * h + 512))
+        mm(v("P%d" % (4 + h), 0, 128), v("VQ", 0, 128), v("VS", 0, 128), eq, es)
+        move(ys, v("P%d" % (4 + h), 0, 128))
+        dma("s", lambda k, h=h: T.oc[:, 512 * h:512 * h + 512], lambda k, x=eq: u8(x), [eq], [], 2100, "st")
+        dma("s", lambda k, h=h: T.y[:, 128 * h:128 * h + 128], lambda k, x=ys: ap(x), [ys], [], 2100, "st")
+    es = fq(R)[1]
     for k in range(4):
-        dma("sa"[k % 2], lambda k=k: T.osc[4 * k:4 * k + 4, 0:256], lambda k=k: T.FS[32 * k:32 * k + 4, 256 * R:256 * R + 256],
-            [es], [], 2000, "st")
-    dma("s", lambda: T.y[:], lambda: T.YS[:], [v("YS", 0, 256)], [], 2200, "st")
-    dma("s", lambda: T.om[:], lambda: T.TO[0:128:16, 0:256], [v("TO", 0, 256)], [], 2000, "st")
-    return ops, sum(sends)
+        dma("sa"[k % 2], lambda _, k=k: T.osc[4 * k:4 * k + 4, 0:256],
+            lambda _, k=k: T.FS[32 * k:32 * k + 4, es[1]:es[2]], [es], [], 2000, "st")
+    dma("s", lambda k: T.om[:], lambda k: T.TO[0:128:16, 0:256], [v("TO", 0, 256)], [], 2000, "st")
+    return ops, R * len(topo.engines(core, to[0]))
 
 
 def rank_program(g, core, T, topo):
@@ -548,26 +570,24 @@ def rank_program(g, core, T, topo):
     if rank is None:
         for i in range(n):
             a, b = cores[i], cores[(i + 1) % n]
-            if _relay(topo, cores, a, b) != core:
+            via = _relay(topo, cores, a, b)
+            if core not in via:
                 continue
             rid, pid = topo.addr(b, core)
-            i0, i1 = _halves(topo, a, core)
-            e0, e1 = _halves(topo, core, b)
             for r in range(R):
-                lo = 160 * r + 128
-                g.wait_ge(T.sem["ac%d" % r], len(i0))
-                g.remote_dma(T.LC[:, lo:lo + 32].bitcast(dt.uint8), T.RC[:, 32 * r:32 * r + 32].bitcast(dt.uint8),
-                             T.sem["ac%d" % r], T.sem.sent, pid, rid, _mask(e0))
-                g.wait_ge(T.sem["as%d" % r], len(i1))
-                g.remote_dma(T.LS[:, lo:lo + 32], T.RS[:, 32 * r:32 * r + 32],
-                             T.sem["as%d" % r], T.sem.sent, pid, rid, _mask(e1))
-            g.wait_ge(T.sem.sent, R * (len(e0) + len(e1)))
+                g.wait_ge(T.sem["ac%d" % r], len(topo.engines(a, core)) // 2)
+                if core == via[0]:
+                    out, in_ = T.FQ[:, CW * r:CW * r + K].bitcast(dt.uint8), T.RC[:, K * r:K * r + K].bitcast(dt.uint8)
+                else:
+                    out, in_ = T.FS[:, SW * r + 128 - K:SW * r + 128], T.RS[:, 128 * r + 128 - K:128 * r + 128]
+                g.remote_dma(out, in_, T.sem["ac%d" % r], T.sem.sent, pid, rid, topo.mask(core, b))
+            g.wait_ge(T.sem.sent, R * len(topo.engines(core, b)))
         return
     nxt, prv = cores[(rank + 1) % n], cores[(rank - 1) % n]
     via = _relay(topo, cores, core, nxt)
     frm = _relay(topo, cores, prv, core)
-    i0, i1 = _halves(topo, prv if frm is None else frm, core)
-    ops, sent = _calls(g, T, nxt if via is None else via, topo, core, via is None)
+    came = len(topo.engines(prv, core)) if core in frm else sum(len(topo.engines(x, core)) for x in frm)
+    ops, sent = _calls(g, T, via, topo, core, nxt in via)
     deps, (_, order, way, at) = _plan(ops)
     queue = {"v": g.vector, "a": g.scalar, "t": g.tensor, "g": g, "s": g.sync}
     count = {"v": 0, "a": 0, "t": 0, "g": 0, "st": 0}
@@ -576,7 +596,7 @@ def rank_program(g, core, T, topo):
         o = ops[i]
         q, _, emit = o["ways"][way[i]]
         if o["kind"] == "n":
-            o["done"] = {"ac%d" % o["round"]: len(i0), "as%d" % o["round"]: len(i1)}
+            o["done"] = {"ac%d" % o["round"]: came}
             o["knew"] = {}
             continue
         kn, need = known[q], {}
@@ -597,8 +617,9 @@ def rank_program(g, core, T, topo):
         if o["kind"] == "r":
             o["done"] = {}
         elif o["kind"] == "d":
-            ins.then_inc(T.sem[o["sem"]], 16)
-            count[o["sem"]] = count.get(o["sem"], 0) + 16
+            for x in ins:
+                x.then_inc(T.sem[o["sem"]], 16)
+            count[o["sem"]] = count.get(o["sem"], 0) + 16 * len(ins)
             o["done"] = {o["sem"]: count[o["sem"]]}
         else:
             count[q] += 1

@@ -3,18 +3,20 @@ from concourse.bass import DstId, RemoteDMATransfer
 from concourse.mybir import dt, AluOpType, AxisListType, ActivationFunctionType
 
 R, P, K, A = 3, 256, 32, 96
-ROWS = [[9, 7], [9, 7], [9, 7]]
+ROWS = [[9, 8], [9, 8], [9, 8]]
 AM = 12
-SAME, CROSS, RING, PERIOD = 60, 100, 5000.0, 19000.0
+SAME, CROSS, RING, PERIOD = 200, 200, 3500.0, 18000.0
 DUE = {"setup": 9e4, "start": 0, "lay0": 1300, "rows0": 5800, "send": 7800, "lay1": 4500, "source": 12000,
        "rows1": 12700, "writers": 14200, "keepers": 14000, "count": 16000, "free": 19000, "layer": 19000, "copy": 23000}
-SEED, TRIES, WARM, MIX = 1, 900000, 80.0, 0.5
+LAT, LEAN, PULL = 500.0, 0.05, 0.03
+CYCLE, FIX, FLOOR = 0.92, 0.0, 64.0
+SEED, TRIES, WARM, MIX = 7, 1000000, 60.0, 0.5
 DS, HS = 256, 384
 WN = HS + A
 BIG = 1e29
 HOLD = 1024.0
 BF, F16, F32, I32, U16, CODE, U8 = "bfloat16", "float16", "float32", "int32", "uint16", "float8_e4m3fn_x4", "uint8"
-FLW, SCW = 256 * AM, 128 * AM + 16
+FLW, SCW = 258 * AM, 129 * AM + 16
 CW, SW, PW = K + P, 128 + P, A + 1024
 TWN = 4 * WN
 
@@ -32,11 +34,11 @@ SCRATCH = {
     "BT": _sb(512, BF), "BQ": _sb(128 * R, CODE), "BS": _sb(128 * R, U8),
     "RC": _sb(32 * R, CODE), "RS": _sb(128 * R, U8),
     "ZT": _sb(512, BF), "ZQ": _sb(128, CODE), "ZS": _sb(128, U8), "RB": _sb(4 * A, F32),
-    "IOF": _sb(256, F32), "IOB": _sb(HS, BF), "IOP": _sb(256, BF), "N16": _sb(256, BF), "CI": _sb(24, I32),
+    "IOB": _sb(HS, BF), "N16": _sb(256, BF), "CI": _sb(24, I32),
     "CF": _sb(64, F32), "UL": _sb(16, U16), "MK": _sb(256, BF), "DM": _sb(256, F32),
-    "KH": _sb(256, F32), "KX": _sb(400, BF), "K4": _sb(4 * A, BF), "DK": _sb(256 * 4, BF),
-    "G16": _sb(3 * 272, BF), "HU": _sb(2 * 272, BF), "HW": _sb(6 * 256, BF),
-    "ZZ": _sb(1024, F32), "TA": _sb(512, F32), "D1": _sb(512, F32), "HF": _sb(512, F32),
+    "KH": _sb(256, F32), "KX": _sb(128, BF), "K4": _sb(4 * A, BF), "DK": _sb(256, BF),
+    "G16": _sb(3 * 272 + 128, BF), "HU": _sb(2 * 272, BF), "HW": _sb(6 * 256, BF), "IOP": _sb(256, BF),
+    "TA": _sb(512, F32), "ZZ": _sb(1024, F32), "D1": _sb(512, F32), "HF": _sb(512, F32),
     "FL": _sb(2 * FLW, F16), "SC": _sb(2 * SCW, F16), "SG": _sb(2 * 4096, BF), "FD": _sb(1024, F16),
     "RI": _sb(64 * R, I32), "SM": _sb(512 * R, F32), "LI": _sb(208 * R + 80, U16),
     "OF": _sb(256, BF), "OM": _sb(160, F16), "S1": _sb(256, BF), "ZF": _sb(256, BF), "ZM": _sb(2 * A, F16),
@@ -121,6 +123,7 @@ def _plan(ops):
             late[j] = min(late[j], late[i] - 1.0)
     ways = [[("vatgsn".index(w[0]), w[1]) for w in o["ways"]] for o in ops]
     lat = [o["lat"] for o in ops]
+    marks = [i for i, o in enumerate(ops) if o["kind"] == "r" or o["kin"] == "start"]
 
     def times(order, way, lo, hi, at, end, on, free):
         for i in order[lo:hi]:
@@ -145,7 +148,7 @@ def _plan(ops):
         if t % 200 == 0:
             times(order, way, 0, n, at, end, on, [0.0] * 6)
             order = sorted(order, key=lambda i: (at[i], i))
-            now = max(end) + MIX * sum(at) / n
+            now = max(end) + MIX * sum(at) / n + PULL * sum(at[j] for j in marks)
             if max(end) < best[0]:
                 best = (max(end), order, way, list(at))
         p = k = draw(n)
@@ -167,6 +170,8 @@ def _plan(ops):
                 continue
             o2.insert(k, i)
         room = -(WARM * (1.0 - t / TRIES) + 1.0) * math.log((1.0 + draw(65536)) / 65536.0)
+        if flip:
+            room += LEAN * ways[i][0][1] * (1 if w2[i] else -1)
         a2, e2, n2, free = list(at), list(end), list(on), [0.0] * 6
         lo, hi = min(p, k), max(p, k) + 50
         for j in order[max(0, lo - 30):lo] if ways[i][0][0] < 2 else order[:lo]:
@@ -177,7 +182,7 @@ def _plan(ops):
             continue
         if any(moved):
             times(o2, w2, hi, n, a2, e2, n2, free)
-        new = max(e2) + MIX * sum(a2) / n
+        new = max(e2) + MIX * sum(a2) / n + PULL * sum(a2[j] for j in marks)
         if new - now <= room:
             now, order, way, at, end, on = new, o2, w2, a2, e2, n2
     PLAN["p"] = (deps, best)
@@ -229,35 +234,42 @@ def _calls(g, T, to, topo, core, land):
         ops[-1]["ways"] += o["ways"]
         ops[-1]["r"] = ops[-1]["r"] + o["r"]
 
-    def rate(o, x):
-        return 1.56 if x[0] == "ind" else 0.5 if two(o, x) else 1.0
+    def together():
+        o = ops.pop()
+        (q, c0, e0), (_, c1, e1) = ops[-1]["ways"][0], o["ways"][0]
+        ops[-1].update(ways=[(q, c0 + c1, lambda: [e0(), e1()])], r=ops[-1]["r"] + o["r"], w=ops[-1]["w"] + o["w"])
+
+    def cost(o, *xs, by=0.0):
+        if "ind" in (o[0], xs[0][0]):
+            return CYCLE * (70 + size(o) * (3.8 if o[0] == "ind" else 1.56))
+        return CYCLE * (FIX + max(FLOOR, size(o) * (by or (0.5 if two(o, *xs) else 1.0))))
 
     def ts(o, x, s1, op0, s2=None, op1=None):
         def e():
             if op1 is None:
                 return g.vector.tensor_scalar(ap(o), ap(x), ap(s1), None, op0)
             return g.vector.tensor_scalar(ap(o), ap(x), ap(s1), ap(s2), op0, op1)
-        add("v", 55 + size(o) * rate(o, x), regs(x, s1, s2), [o], e)
+        add("v", cost(o, x), regs(x, s1, s2), [o], e)
 
     def tt(o, x, y, op):
         k = 1.0 if SCRATCH[x[0]][0] == "psum" else 2.0
-        add("v", 55 + size(o) * k, regs(x, y), [o], lambda: g.vector.tensor_tensor(ap(o), ap(x), ap(y), op))
+        add("v", cost(o, x, by=k), regs(x, y), [o], lambda: g.vector.tensor_tensor(ap(o), ap(x), ap(y), op))
 
     def cp(o, x):
         if o[0] == "ind":
-            add("v", 55 + size(x) * 3.8, [x, o[2]], [o[1]], lambda: g.vector.tensor_copy(ap(o), ap(x)))
+            add("v", cost(o, x), [x, o[2]], [o[1]], lambda: g.vector.tensor_copy(ap(o), ap(x)))
         else:
-            add("v", 55 + size(o) * rate(o, x), regs(x), [o], lambda: g.vector.tensor_copy(ap(o), ap(x)))
+            add("v", cost(o, x), regs(x), [o], lambda: g.vector.tensor_copy(ap(o), ap(x)))
 
     def scan(o, d0, d1, op0, op1, first=0.0):
-        add("v", 55 + size(o) * (0.5 if two(o, d0, d1) else 1.0), [d0, d1], [o],
+        add("v", cost(o, d0, d1), [d0, d1], [o],
             lambda: g.vector.tensor_tensor_scan(ap(o), ap(d0), ap(d1), first, op0, op1))
 
     def hold(o, x, k="KX"):
         scan(o, v(k, 0, size(x)), x, Op.add, Op.max)
 
     def fill(o, c):
-        add("v", 55 + size(o) * (0.5 if two(o) else 1.0), [], [o], lambda: g.vector.memset(ap(o), c))
+        add("v", cost(o, o), [], [o], lambda: g.vector.memset(ap(o), c))
 
     def act(o, x, f, bias=None, scale=None, acc=None):
         def e():
@@ -269,7 +281,7 @@ def _calls(g, T, to, topo, core, land):
             if acc is not None:
                 kw["accum_out"] = ap(acc)
             return g.scalar.activation(ap(o), ap(x), f, **kw)
-        add("a", 70 + (20 if acc else 0) + size(o) * (1.56 if x[0] == "ind" else 1.0), regs(x, bias),
+        add("a", 10 + (20 if acc else 0) + cost(o, x, by=1.0), regs(x, bias),
             [o] + ([acc] if acc else []), e)
 
     def move(o, x):
@@ -285,13 +297,8 @@ def _calls(g, T, to, topo, core, land):
         act(o, x, Fn.Relu if relu else Fn.Identity, bias=None if relu else b, scale=a)
         either()
 
-    def nil(o, x, a):
-        ts(o, x, 0.0, Op.is_equal, a, Op.mult)
-        act(o, x, Fn.Relu, bias=a, scale=-a)
-        either()
-
     def quant(c, s, x):
-        add("v", 30 + size(x) * 0.27, [x], [c, s], lambda: g.vector.quantize_mx(ap(c), ap(s), ap(x)))
+        add("v", CYCLE * (20 + size(x) * 0.265), [x], [c, s], lambda: g.vector.quantize_mx(ap(c), ap(s), ap(x)))
 
     def mm(o, a, b, c, d):
         add("t", (size(o) + 16) * 0.65, [a, b, c, d], [v(o[0], 0, 512)],
@@ -302,17 +309,17 @@ def _calls(g, T, to, topo, core, land):
             if SCRATCH[o[0]][2] == I32:
                 return g.iota(ap(o), pat, base, cm)
             return g.iota(ap(o), pat, base, cm, allow_small_or_imprecise_dtypes=True)
-        add("g", 150 + 2 * size(o), [], [o], e)
+        add("g", 180 + 2.4 * size(o), [], [o], e)
 
     def keep(o, x, pat, op, other, base, cm, on=ap):
-        add("g", 190 + 2 * size(o), [x], [o], lambda: g.affine_select(on(o), on(x), pat, op, other, base, cm))
+        add("g", 230 + 2.4 * size(o), [x], [o], lambda: g.affine_select(on(o), on(x), pat, op, other, base, cm))
 
     def dma(q, out, in_, r, w, lat, sem=None, times=1):
         if sem is None:
             sem = "d%d" % nd[0]
             nd[0] += 1
         eng = g.sync if q == "s" else g.scalar
-        i = add(q, 80 * times, r, w, lambda: [eng.dma_start(out(k), in_(k)) for k in range(times)], lat=lat, kind="d")
+        i = add(q, 80 * times, r, w, lambda: [eng.dma_start(out(k), in_(k)) for k in range(times)], lat=lat - LAT, kind="d")
         ops[i]["sem"] = sem
 
     def copy(o, x):
@@ -339,23 +346,20 @@ def _calls(g, T, to, topo, core, land):
     iota(v("CI", 0, 1), [[0, 1]], 0, 1)
     iota(v("N16", 0, 256), [[0, 16], [1, 16]])
     iota(v("CI", 8, 24), [[1, 2], [16, 8]])
-    iota(v("IOF", 0, 256), [[1, 256]])
     iota(v("IOB", 0, HS), [[1, HS]])
     iota(v("IOP", 0, 256), [[1, 16], [16, 16]], 1)
     iota(v("K4", A, 2 * A), [[0, A // 4], [1, 4]])
     for h in range(4):
         keep(v("ET", 512 * h, 512 * h + 512), v("ZERO", 0, 512), [[-4, 128], [-1, 4]], Op.not_equal, 1.0, h, 4)
-    dk = {}
-    for a in sorted(set(sum(ROWS, []))):
-        b = dk[a] = 256 * len(dk)
-        iota(v("DK", b, b + 16 * (16 - a)), [[0, 16 - a], [1024, 16]])
-        iota(v("DK", b + 16 * (16 - a), b + 256), [[0, a], [1024, 16]], -128)
+    line(v("DK", 0, 256), v("N16", 0, 256), HOLD, 0.0)
     for d in range(3):
         keep(v("G16", 0, 272), v("G16" if d else "ZERO", 0, 272), [[-1, 272]], Op.not_equal, 256.0 ** d, 15 + d, 16, group)
     iota(v("G16", 544, 816), [[0, 16], [1, 17]])
     keep(v("G16", 272, 544), v("G16", 544, 816), [[-1, 16], [0, 17]], Op.is_gt, 0.0, 0, 1, group)
-    dma("s", lambda k: group(v("HU", 0, 544), k), lambda k: group(v("G16", 0, 544)), [v("G16", 0, 544)],
-        [v("HU", 0, 544)], 2500, times=8)
+    for d, x in enumerate((-4 * HOLD, HOLD)):
+        keep(v("G16", 816, 944), v("G16", 816, 944) if d else v("ZERO", 0, 128), [[0, 8], [-1, 16]], Op.not_equal, x, d, 1, group)
+    for o, x in ((v("HU", 0, 544), v("G16", 0, 544)), (v("KX", 0, 128), v("G16", 816, 944))):
+        dma("s", lambda k, o=o: group(o, k), lambda k, x=x: group(x), [x], [o], 2500, times=8)
     for b in range(6):
         copy(v("HW", 256 * b, 256 * b + 256), v("HU", 15 - 3 * b, 271 - 3 * b))
     ts(v("CI", 1, 2), v("CI", 0, 1), 15, Op.bitwise_and)
@@ -370,14 +374,11 @@ def _calls(g, T, to, topo, core, land):
     line(v("KH", 0, 256), v("MK", 0, 256), 3 * BIG, 0.0)
     fill(v("KH", 0, 256, 16), 3 * BIG)
     for o in range(2):
-        cp(v("SC", SCW * o, SCW * o + 1), v("ZERO", 0, 1))
+        ts(v("SC", SCW * o, SCW * o + 1), v("ZERO", 0, 1), -HOLD, Op.add)
+        cp(v("FL", FLW * o + 257, FLW * (o + 1), 258), v("ZERO", 0, AM))
     fill(v("TB", 0, 1), 0.0)
     ts(hq, q, 15.0, Op.is_lt, -HOLD, Op.mult)
     line(hq4, hq, 4.0, 0.0)
-    fill(v("KX", 128, 129), 0.0)
-    line(v("KX", 129, 257), v("MK", 0, 128), HOLD, 0.0)
-    line(v("KX", 272, 400), v("MK", 0, 128), -4 * HOLD, 0.0)
-    tt(v("KX", 0, 128), v("KX", 128, 256), v("KX", 272, 400), Op.add)
     line(qh1, qh, 1.0, 1.0)
     ts(h4, qh, 3.0, Op.is_lt, -4 * HOLD, Op.mult)
     line(hb, h4, 1.0, ql)
@@ -386,17 +387,18 @@ def _calls(g, T, to, topo, core, land):
     tt(v("K4", 0, A), v("K4", 2 * A, 3 * A), v("K4", 3 * A, 4 * A), Op.add)
     line(hm, hq, 1.0, -1.0)
     line(h127, hq, 1.0, 127.0)
+    ts(JW, v("IOB", 0, 256, 16), q, Op.add, -float(HS), Op.add)
     line(q16, q, 16.0, -255.0)
     line(q17, q, 17.0, 0.0)
-    ts(JW, v("IOF", 0, 256, 16), q, Op.add, -float(HS), Op.add)
-    line(PC, v("IOF", 0, 16), 1.0, q16)
-    ts(KC, v("IOF", 0, A, 16), q, Op.add, h127, Op.subtract)
+    line(PC, v("IOB", 0, 16), 1.0, q16)
+    ts(KC, v("IOB", 0, A, 16), q, Op.add, h127, Op.subtract)
     quant(v("EQ", 0, 512), v("ES", 0, 512), v("ET", 0, 2048))
     quant(v("UQ", 0, 128), v("US", 0, 128), v("UT", 0, 512))
-    ul = v("UL", 0, 16)
-    add("v", 455, [v("UQ", 0, 128), ul], [v("UP", 0, 256)], lambda: g.vector.tensor_copy(
-        T.UP[:, 0:256].bitcast(dt.uint32), T.UQ[:, 0:128].bitcast(dt.uint32).indirect(ap(ul))))
-    move(v("UPS", 0, 256), ind(v("US", 0, 128), ul))
+    for o in range(2):
+        ul, up = v("UL", 8 * o, 8 * o + 8), v("UP", 128 * o, 128 * o + 128)
+        add("v", cost(up, ind(up, ul)), [v("UQ", 0, 128), ul], [up], lambda ul=ul, up=up: g.vector.tensor_copy(
+            ap(up).bitcast(dt.uint32), T.UQ[:, 0:128].bitcast(dt.uint32).indirect(ap(ul))))
+        move(v("UPS", 128 * o, 128 * o + 128), ind(v("US", 0, 128), ul))
     quant(v("VQ", 0, 128), v("VS", 0, 128), v("VT", 0, 512))
     l0 = 208 * R
     for t in range(4):
@@ -404,7 +406,7 @@ def _calls(g, T, to, topo, core, land):
         move(v("WA", t, 1024, 4), ind(v("M0", 0, 1024), v("LI", l0 + 16 * t, l0 + 16 * t + 16)))
     p16 = v("LI", l0 + 64, l0 + 80)
     cp(p16, v("PT", 0, 16))
-    line(v("TW", 0, 1024, 4), ind(v("IOF", 0, 256), p16), 1.0, 1.0)
+    line(v("TW", 0, 1024, 4), ind(v("IOB", 0, 256), p16), 1.0, 1.0)
 
     def ranks(r, o, out):
         a = ROWS[r][o]
@@ -416,28 +418,38 @@ def _calls(g, T, to, topo, core, land):
         mm(pv, *side)
         z, b, fl, sc, fd = 512 * o, 256 * o, FLW * o, SCW * o, 512 * o
         hf = v("HF", b, b + 256)
-        act(v("TA", b, b + 256), pa, Fn.Abs, bias=2.0 ** -125, scale=1.0625 * 2.0 ** -24)
-        act(v("ZZ", z + 16, z + 256), v(pa[0], 16, 256), Fn.Copy)
         tt(v("D1", b, b + 256), pv, v("DM", 0, 256), Op.max)
         scan(hf, v("KH", 0, 256), v("D1", b, b + 256), Op.add, Op.min)
-        tt(v("ZZ", z + 256, z + 512), pv, v("TA", b, b + 256), Op.add)
+        m = 16 * n
+        act(v("TA", b, b + m), v(pa[0], 0, m), Fn.Abs, bias=2.0 ** -125, scale=1.0625 * 2.0 ** -24)
+        act(v("ZZ", z + 16, z + 256), v(pa[0], 16, 256), Fn.Copy)
+        tt(v("ZZ", z + 256, z + 256 + m), v(pv[0], 0, m), v("TA", b, b + m), Op.add)
         due[1] = "rows%d" % o
         tt(v("FD", fd, fd + 256), pv, hf, Op.is_equal)
-        scan(v("FD", fd + 256, fd + 512), v("DK", dk[a], dk[a] + 256), v("FD", fd, fd + 256), Op.min, Op.add)
+        scan(v("FD", fd + 256, fd + 512), v("DK", 0, 256), v("FD", fd, fd + 256), Op.min, Op.add)
         acc = 512 * r + 16 * o
         for c in range(16):
             win, s = v("ZZ", z + 16 * c + 16, z + 16 * c + 272), v("HF", b + 16 * c + 15, b + 16 * c + 16)
+            cut = 16 * c + 16
             if c >= n:
-                ts(v("FL", fl + 256 * (c - n), fl + 256 * (c - n + 1)), win, s, Op.is_gt, -0.5, Op.add)
+                x = fl + 258 * (c - n)
+                ts(v("FL", x, x + cut), v(pv[0], 0, cut), s, Op.is_ge, -0.5, Op.add)
+                if cut < 256:
+                    ts(v("FL", x + cut, x + 256), v(pv[0], cut, 256), s, Op.is_gt, -0.5, Op.add)
+                    together()
             else:
                 sg = v("SG", 4096 * o + 256 * c, 4096 * o + 256 * c + 256)
                 act(sg, win, Fn.Sign, bias=s, scale=-1.0)
                 act(sg, sg, Fn.Relu, scale=-1.0, acc=v("SM", acc + c, acc + c + 1))
-        w = 128 * a
+        w = 129 * a
+        ts(v("FL", fl + 256, fl + 2 * w, 258), v("FD", fd + 256 + m + 15, fd + 512, 16), -1.0, Op.mult, 128.0, Op.add)
+        ops[-1]["w"] = [v("FL", x, x + 1) for x in range(fl + 256, fl + 2 * w, 258)]
         due[1] = ("send", "writers")[o]
-        scan(v("SC", sc + 1, sc + 1 + w), v("FL", fl, fl + 2 * w, 2), v("FL", fl + 1, fl + 2 * w, 2), Op.add, Op.add)
-        tt(v("SM", acc + n, acc + 16), v("SC", sc + 128, sc + w + 1, 128), v("SC", sc, sc + w - 127, 128), Op.subtract)
-        tt(out, v("SM", acc, acc + 16), v("FD", fd + 256 + 15, fd + 512, 16), Op.subtract)
+        flags = [v("FL", fl, fl + 2 * w)]
+        scan(v("SC", sc + 1, sc + 1 + w), v("FL", fl, fl + 2 * w, 2), v("FL", fl + 1, fl + 2 * w, 2), Op.add, Op.add, -HOLD)
+        ops[-1]["r"] = flags
+        tt(v(out[0], out[1] + n, out[2]), v("SC", sc + 129, sc + w + 1, 129), v("SC", sc, sc + w - 128, 129), Op.subtract)
+        tt(v(out[0], out[1], out[1] + n), v("SM", acc, acc + n), v("FD", fd + 256 + 15, fd + 256 + m, 16), Op.subtract)
 
     for r in range(R):
         W, Wn = ("WA", "WB") if r % 2 == 0 else ("WB", "WA")
@@ -512,15 +524,16 @@ def _calls(g, T, to, topo, core, land):
                      ind(v(W, 0, 4 * WN), L(96 + 16 * t + 8 * h, 16 // parts)))
         due[1] = "count"
         for b in range(6):
-            act(v("HJ", 128 * b, 128 * b + 128), ind(v("HW", 256 * b, 256 * b + 256), L(160, 8)), Fn.Identity, acc=S(80 + b, 1))
+            act(v("HJ", 128 * b, 128 * b + 128), ind(v("HW", 256 * b, 256 * b + 256), L(160, 8)), Fn.Identity,
+                acc=S(80 + b, 1))
         due[1] = "free"
-        dig, cnt = v("RI", ri + 32, ri + 38), v("RI", ri + 40, ri + 56)
-        cp(dig, S(80, 6))
-        ts(v("RI", ri + 40, ri + 58, 3), dig, 255, Op.bitwise_and)
-        ts(v("RI", ri + 41, ri + 58, 3), dig, 8, Op.arith_shift_right, 255, Op.bitwise_and)
-        ts(v("RI", ri + 42, ri + 58, 3), dig, 16, Op.arith_shift_right)
+        dig, cnt = v("RI", ri + 32, ri + 48), v("RI", ri + 48, ri + 64)
+        for d in range(3):
+            line(v("SM", sm + 96 + d, sm + 114, 3), S(80, 6), 256.0 ** -d, -0.25)
+        cp(dig, S(96, 16))
+        ts(cnt, dig, 255, Op.bitwise_and)
         ts(S(128, 16), cnt, 0.0, Op.is_equal)
-        scan(S(144, 16), v("IOF", 0, 16), S(128, 16), Op.min, Op.add)
+        scan(S(144, 16), v("IOB", 0, 16), S(128, 16), Op.min, Op.add)
         ts(L(192, 1), S(159, 1), q17, Op.add)
         act(v("HJ", 768, 784), ind(v("HU", 272, 544), L(192, 1)), Fn.Identity, acc=S(224, 1))
         ts(S(248, 16), cnt, 2.0, Op.min, 512.0, Op.mult)
@@ -536,13 +549,16 @@ def _calls(g, T, to, topo, core, land):
         move(v("WT", wt, wt + A), ind(v("TW", tw, tw + 4 * HS), L(88, 6)))
         hold(v("TF", 0, A), v("WT", wt, wt + A))
         ts(L(184, 6), v("TF", 15, A, 16), hm, Op.add)
-        nil(v("TB", 1, A + 1), ind(v("WT", wt + A + 256, wt + A + 512), L(184, 6)), 128.0)
+        single = ind(v("WT", wt + A + 256, wt + A + 512), L(184, 6))
+        ts(v("TB", 1, A + 1), single, 0.0, Op.is_equal, 128.0, Op.mult)
+        act(v("TB", 1, A + 1), single, Fn.Relu, bias=128.0, scale=-128.0)
+        either()
         line(v("TB", 128, 128 + A), v("TB", 1, A + 1), 129.0 / 128.0, 0.0)
         scan(v("TF", A, 2 * A), v("TB", 128, 128 + A), v("TB", 0, A), Op.add, Op.subtract, -128.0)
         hold(v("TF", 2 * A, 3 * A), v("TF", A, 2 * A))
         tt(S(352, 6), v("TF", 2 * A + 15, 3 * A, 16), KC, Op.max)
-        ts(L(194, 6), S(352, 6), h127, Op.add)
-        move(v("TW", tw + 4 * HS, tw + TWN, 4), ind(v("WT", wt, wt + A + 128), L(194, 6)))
+        ts(L(200, 6), S(352, 6), h127, Op.add)
+        move(v("TW", tw + 4 * HS, tw + TWN, 4), ind(v("WT", wt, wt + A + 128), L(200, 6)))
         if r < R - 1:
             move(v("TW", tn, tn + 1024, 4), ind(v("TW", tw, tw + TWN), L(96, 16)))
         else:
@@ -622,8 +638,9 @@ def rank_program(g, core, T, topo):
             count[o["sem"]] = count.get(o["sem"], 0) + 16 * len(ins)
             o["done"] = {o["sem"]: count[o["sem"]]}
         else:
-            count[q] += 1
-            ins.then_inc(T.sem[q], 1)
+            for x in ins if isinstance(ins, list) else [ins]:
+                count[q] += 1
+                x.then_inc(T.sem[q], 1)
             o["done"] = {q: count[q]}
     for s in count:
         g.wait_ge(T.sem[s], count[s])

import math
from concourse.bass import DstId, RemoteDMATransfer
from concourse.mybir import dt, AluOpType, AxisListType, ActivationFunctionType

R, P, K, A = 3, 256, 32, 96
ROWS = [[9, 8], [9, 8], [9, 8]]
AM = 12
SAME, CROSS, RING, PERIOD = 200, 200, 3500.0, 18000.0
DUE = {"setup": 9e4, "start": 0, "lay0": 1300, "rows0": 5800, "send": 7800, "lay1": 4500, "source": 12000,
       "rows1": 12700, "writers": 14200, "keepers": 14000, "count": 16000, "free": 19000, "layer": 19000, "copy": 23000}
LAT, LEAN, PULL = 500.0, 0.05, 0.03
CYCLE, FIX, FLOOR = 0.92, 0.0, 64.0
SEED, TRIES, WARM, MIX = 7, 1000000, 60.0, 0.5
DS, HS = 256, 384
WN = HS + A
BIG = 1e29
HOLD = 1024.0
BF, F16, F32, I32, U16, CODE, U8 = "bfloat16", "float16", "float32", "int32", "uint16", "float8_e4m3fn_x4", "uint8"
FLW, SCW = 258 * AM, 129 * AM + 16
CW, SW, PW = K + P, 128 + P, A + 1024
TWN = 4 * WN


def _sb(n, d):
    return ("sbuf", [128, n], d)


SCRATCH = {
    "M0": _sb(1024, BF), "UT": _sb(512, BF), "VT": _sb(512, BF), "PT": _sb(16, I32),
    "WC": _sb(512, CODE), "WS": _sb(512, U8), "UQ": _sb(128, CODE), "US": _sb(128, U8),
    "UP": _sb(256, CODE), "UPS": _sb(256, U8), "VQ": _sb(128, CODE), "VS": _sb(128, U8),
    "ET": _sb(2048, BF), "EQ": _sb(512, CODE), "ES": _sb(512, U8), "ZERO": _sb(1024, BF),
    "WA": _sb(4 * WN, BF), "WB": _sb(4 * WN, BF), "FQ": _sb(CW * 4, CODE), "FS": _sb(SW * 4, U8),
    "BT": _sb(512, BF), "BQ": _sb(128 * R, CODE), "BS": _sb(128 * R, U8),
    "RC": _sb(32 * R, CODE), "RS": _sb(128 * R, U8),
    "ZT": _sb(512, BF), "ZQ": _sb(128, CODE), "ZS": _sb(128, U8), "RB": _sb(4 * A, F32),
    "IOB": _sb(HS, BF), "N16": _sb(256, BF), "CI": _sb(24, I32),
    "CF": _sb(64, F32), "UL": _sb(16, U16), "MK": _sb(256, BF), "DM": _sb(256, F32),
    "KH": _sb(256, F32), "KX": _sb(128, BF), "K4": _sb(4 * A, BF), "DK": _sb(256, BF),
    "G16": _sb(3 * 272 + 128, BF), "HU": _sb(2 * 272, BF), "HW": _sb(6 * 256, BF), "IOP": _sb(256, BF),
    "TA": _sb(512, F32), "ZZ": _sb(1024, F32), "D1": _sb(512, F32), "HF": _sb(512, F32),
    "FL": _sb(2 * FLW, F16), "SC": _sb(2 * SCW, F16), "SG": _sb(2 * 4096, BF), "FD": _sb(1024, F16),
    "RI": _sb(64 * R, I32), "SM": _sb(512 * R, F32), "LI": _sb(208 * R + 80, U16),
    "OF": _sb(256, BF), "OM": _sb(160, F16), "S1": _sb(256, BF), "ZF": _sb(256, BF), "ZM": _sb(2 * A, F16),
    "TW": _sb(2 * TWN, BF), "WT": _sb(PW * R, BF), "TL": _sb(128, BF), "TM": _sb(128, F16), "HJ": _sb(7 * 128, BF),
    "TB": _sb(224, BF), "TF": _sb(3 * A, F16), "TO": _sb(256, F32), "YS": _sb(256, F32),
}
for _i in range(8):
    SCRATCH["P%d" % _i] = ("psum", [128, 512], F32)
SEMAPHORES = ["v", "a", "t", "g", "st", "sent"] + ["d%d" % i for i in range(32)] + ["ac%d" % r for r in range(R)]
PLAN = {}


def _mask(es):
    m = 0
    for e in es:
        m |= 1 << e
    return m


def _relay(topo, cores, a, b):
    if topo.may_write(a, b):
        return [b, b]
    c = [x for x in topo.cores_of(a) if x not in cores and topo.may_write(x, b)]
    c.sort(key=lambda x: topo.die(x) != topo.die(a))
    return c[:2]


def _hop(g, T, topo, core, to, r, codes, scales):
    es = topo.engines(core, to[0])
    h = len(es) // 2
    return g.remote_dma_fused(
        [RemoteDMATransfer(dst_ids=[DstId(rid=topo.addr(b, core)[0], pnc=topo.addr(b, core)[1])], src=x, dst=o,
                           dma_engine_mask=_mask(e), remote_sem=T.sem["ac%d" % r])
         for b, e, (o, x) in zip(to, (es[:h], es[h:]), (codes, scales))], local_sem=T.sem.sent)


def _overlap(x, y):
    if x[0] != y[0] or x[1] >= y[2] or y[1] >= x[2]:
        return False
    if x[3] == y[3] and x[3] > 1 and (x[1] - y[1]) % x[3]:
        return False
    return True


def _deps(ops):
    out, above = [], []
    for i, o in enumerate(ops):
        d, seen = [], 0
        for j in range(i - 1, -1, -1):
            if seen >> j & 1:
                continue
            p = ops[j]
            hit = j in o["after"]
            for w in p["w"]:
                if any(_overlap(w, x) for x in o["r"]) or any(_overlap(w, x) for x in o["w"]):
                    hit = True
            for x in p["r"]:
                if any(_overlap(x, w) for w in o["w"]):
                    hit = True
                if SCRATCH[x[0]][0] == "psum" and any(y[0] == x[0] for y in o["r"]) and \
                        (len(p["ways"]) > 1 or len(o["ways"]) > 1 or p["ways"][0][0] != o["ways"][0][0]):
                    hit = True
            if hit:
                d.append(j)
                seen |= above[j] | 1 << j
        out.append(d)
        above.append(seen if o["kind"] in "cd" else 0)
    return out


def _plan(ops):
    if "p" in PLAN:
        return PLAN["p"]
    deps = _deps(ops)
    n = len(ops)
    succ = [[] for _ in ops]
    late = [o["due"] for o in ops]
    for i in range(n - 1, -1, -1):
        late[i] -= ops[i]["ways"][-1][1] + ops[i]["lat"]
        for j in deps[i]:
            succ[j].append(i)
            late[j] = min(late[j], late[i] - 1.0)
    ways = [[("vatgsn".index(w[0]), w[1]) for w in o["ways"]] for o in ops]
    lat = [o["lat"] for o in ops]
    marks = [i for i, o in enumerate(ops) if o["kind"] == "r" or o["kin"] == "start"]

    def times(order, way, lo, hi, at, end, on, free):
        for i in order[lo:hi]:
            q, c = ways[i][way[i]]
            t = free[q]
            for d in deps[i]:
                e = end[d] + (SAME if on[d] == q else CROSS)
                if e > t:
                    t = e
            at[i], free[q], end[i], on[i] = t, t + c, t + c + lat[i], q

    x = [SEED]

    def draw(k):
        x[0] = (x[0] * 1103515245 + 12345) % 2147483648
        return (x[0] >> 8) % k

    order, way = sorted(range(n), key=lambda i: late[i]), [len(w) - 1 for w in ways]
    at, end, on = [0.0] * n, [0.0] * n, [0] * n
    best = (1e9,)
    for t in range(TRIES):
        if t % 200 == 0:
            times(order, way, 0, n, at, end, on, [0.0] * 6)
            order = sorted(order, key=lambda i: (at[i], i))
            now = max(end) + MIX * sum(at) / n + PULL * sum(at[j] for j in marks)
            if max(end) < best[0]:
                best = (max(end), order, way, list(at))
        p = k = draw(n)
        i, o2, w2 = order[p], order, way
        flip = len(ways[i]) > 1 and draw(10) < 3
        if flip:
            w2 = list(way)
            w2[i] = 1 - w2[i]
        if not flip or draw(2):
            far = 1 + draw((2, 8, 20, 60)[draw(4)])
            o2 = order[:p] + order[p + 1:]
            if draw(2):
                while k > max(0, p - far) and o2[k - 1] not in deps[i]:
                    k -= 1
            else:
                while k < min(n - 1, p + far) and o2[k] not in succ[i]:
                    k += 1
            if k == p and not flip:
                continue
            o2.insert(k, i)
        room = -(WARM * (1.0 - t / TRIES) + 1.0) * math.log((1.0 + draw(65536)) / 65536.0)
        if flip:
            room += LEAN * ways[i][0][1] * (1 if w2[i] else -1)
        a2, e2, n2, free = list(at), list(end), list(on), [0.0] * 6
        lo, hi = min(p, k), max(p, k) + 50
        for j in order[max(0, lo - 30):lo] if ways[i][0][0] < 2 else order[:lo]:
            free[on[j]] = end[j] - lat[j]
        times(o2, w2, lo, hi, a2, e2, n2, free)
        moved = [a2[j] - at[j] for j in o2[hi - 25:hi]]
        if moved and min(moved) > room:
            continue
        if any(moved):
            times(o2, w2, hi, n, a2, e2, n2, free)
        new = max(e2) + MIX * sum(a2) / n + PULL * sum(a2[j] for j in marks)
        if new - now <= room:
            now, order, way, at, end, on = new, o2, w2, a2, e2, n2
    PLAN["p"] = (deps, best)
    return PLAN["p"]


def _calls(g, T, to, topo, core, land):
    Op, Fn = AluOpType, ActivationFunctionType
    ops = []
    nd = [0]
    due = [0.0, "setup"]

    def v(name, lo, hi, st=1):
        return (name, lo, hi, st)

    def ap(x):
        if isinstance(x, tuple) and x[0] == "ind":
            return ap(x[1]).indirect(ap(x[2]))
        if isinstance(x, tuple):
            return T[x[0]][:, x[1]:x[2]:x[3]] if x[3] > 1 else T[x[0]][:, x[1]:x[2]]
        return x

    def group(x, k=0):
        return T[x[0]][16 * k:16 * k + 16, x[1]:x[2]]

    def ind(w, o):
        return ("ind", w, o)

    def regs(*xs):
        out = []
        for x in xs:
            if isinstance(x, tuple):
                out += [x[1], x[2]] if x[0] == "ind" else [x]
        return out

    def size(x):
        return 16 * size(x[2]) if x[0] == "ind" else (x[2] - x[1] + x[3] - 1) // x[3]

    def two(*xs):
        return all(x[0] != "ind" and SCRATCH[x[0]][2] in (BF, F16, U16) for x in xs)

    def add(q, cost, r, w, emit, lat=0.0, kind="c", after=()):
        ops.append({"ways": [(q, cost, emit)], "lat": lat, "r": r, "w": w, "kind": kind, "after": list(after),
                    "kin": due[1], "due": due[0] + DUE[due[1]]})
        return len(ops) - 1

    def either():
        o = ops.pop()
        ops[-1]["ways"] += o["ways"]
        ops[-1]["r"] = ops[-1]["r"] + o["r"]

    def together():
        o = ops.pop()
        (q, c0, e0), (_, c1, e1) = ops[-1]["ways"][0], o["ways"][0]
        ops[-1].update(ways=[(q, c0 + c1, lambda: [e0(), e1()])], r=ops[-1]["r"] + o["r"], w=ops[-1]["w"] + o["w"])

    def cost(o, *xs, by=0.0):
        if "ind" in (o[0], xs[0][0]):
            return CYCLE * (70 + size(o) * (3.8 if o[0] == "ind" else 1.56))
        return CYCLE * (FIX + max(FLOOR, size(o) * (by or (0.5 if two(o, *xs) else 1.0))))

    def ts(o, x, s1, op0, s2=None, op1=None):
        def e():
            if op1 is None:
                return g.vector.tensor_scalar(ap(o), ap(x), ap(s1), None, op0)
            return g.vector.tensor_scalar(ap(o), ap(x), ap(s1), ap(s2), op0, op1)
        add("v", cost(o, x), regs(x, s1, s2), [o], e)

    def tt(o, x, y, op):
        k = 1.0 if SCRATCH[x[0]][0] == "psum" else 2.0
        add("v", cost(o, x, by=k), regs(x, y), [o], lambda: g.vector.tensor_tensor(ap(o), ap(x), ap(y), op))

    def cp(o, x):
        if o[0] == "ind":
            add("v", cost(o, x), [x, o[2]], [o[1]], lambda: g.vector.tensor_copy(ap(o), ap(x)))
        else:
            add("v", cost(o, x), regs(x), [o], lambda: g.vector.tensor_copy(ap(o), ap(x)))

    def scan(o, d0, d1, op0, op1, first=0.0):
        add("v", cost(o, d0, d1), [d0, d1], [o],
            lambda: g.vector.tensor_tensor_scan(ap(o), ap(d0), ap(d1), first, op0, op1))

    def hold(o, x, k="KX"):
        scan(o, v(k, 0, size(x)), x, Op.add, Op.max)

    def fill(o, c):
        add("v", cost(o, o), [], [o], lambda: g.vector.memset(ap(o), c))

    def act(o, x, f, bias=None, scale=None, acc=None):
        def e():
            kw = {}
            if bias is not None:
                kw["bias"] = ap(bias)
            if scale is not None:
                kw["scale"] = scale
            if acc is not None:
                kw["accum_out"] = ap(acc)
            return g.scalar.activation(ap(o), ap(x), f, **kw)
        add("a", 10 + (20 if acc else 0) + cost(o, x, by=1.0), regs(x, bias),
            [o] + ([acc] if acc else []), e)

    def move(o, x):
        cp(o, x)
        act(o, x, Fn.Copy)
        either()

    def line(o, x, a, b, relu=False):
        if relu:
            ts(o, x, 0.0, Op.max, a, Op.mult)
        else:
            ts(o, x, a, Op.mult, b, Op.add)
        act(o, x, Fn.Relu if relu else Fn.Identity, bias=None if relu else b, scale=a)
        either()

    def quant(c, s, x):
        add("v", CYCLE * (20 + size(x) * 0.265), [x], [c, s], lambda: g.vector.quantize_mx(ap(c), ap(s), ap(x)))

    def mm(o, a, b, c, d):
        add("t", (size(o) + 16) * 0.65, [a, b, c, d], [v(o[0], 0, 512)],
            lambda: g.tensor.matmul_mx(ap(o), ap(a), ap(b), ap(c), ap(d), True, True), lat=100.0)

    def iota(o, pat, base=0, cm=0):
        def e():
            if SCRATCH[o[0]][2] == I32:
                return g.iota(ap(o), pat, base, cm)
            return g.iota(ap(o), pat, base, cm, allow_small_or_imprecise_dtypes=True)
        add("g", 180 + 2.4 * size(o), [], [o], e)

    def keep(o, x, pat, op, other, base, cm, on=ap):
        add("g", 230 + 2.4 * size(o), [x], [o], lambda: g.affine_select(on(o), on(x), pat, op, other, base, cm))

    def dma(q, out, in_, r, w, lat, sem=None, times=1):
        if sem is None:
            sem = "d%d" % nd[0]
            nd[0] += 1
        eng = g.sync if q == "s" else g.scalar
        i = add(q, 80 * times, r, w, lambda: [eng.dma_start(out(k), in_(k)) for k in range(times)], lat=lat - LAT, kind="d")
        ops[i]["sem"] = sem

    def copy(o, x):
        dma("s", lambda k: ap(o), lambda k: ap(x), [x] + m0, [o], 2500)

    def u8(x):
        return ap(x).bitcast(dt.uint8)

    def fq(r, lo=K, n=P):
        return v("FQ", CW * r + lo, CW * r + lo + n), v("FS", SW * r + 128 - K + lo, SW * r + 128 - K + lo + n)

    dma("s", lambda k: T.M0[:], lambda k: T.m[:], [], [v("M0", 0, 1024)], 2600)
    dma("a", lambda k: T.PT[:], lambda k: T.pt[:], [], [v("PT", 0, 16)], 2000)
    dma("a", lambda k: T.UT[:], lambda k: T.u[:], [], [v("UT", 0, 512)], 2400)
    m0 = [v("M0", 0, 1024)]
    dma("s", lambda k: T.WC[:].bitcast(dt.uint8), lambda k: T.wc[:], m0, [v("WC", 0, 512)], 3000)
    dma("s", lambda k: T.WS[:], lambda k: T.ws[:], m0, [v("WS", 0, 512)], 3000)
    dma("s", lambda k: T.VT[:], lambda k: T.v[:], m0, [v("VT", 0, 512)], 3000)
    fill(v("ZERO", 0, 1024), 0.0)
    for x in [v("TW", TWN // 2 * h, TWN // 2 * (h + 1)) for h in range(4)] + \
            [v("BT", 0, 384), v("ZT", 4 * A, 512), v("WA", 4 * DS, 4 * HS), v("WB", 4 * DS, 4 * HS)] + \
            [v("WT", PW * r + A + 256, PW * r + A + 512) for r in range(R)]:
        copy(x, v("ZERO", 0, size(x)))
    iota(v("CI", 0, 1), [[0, 1]], 0, 1)
    iota(v("N16", 0, 256), [[0, 16], [1, 16]])
    iota(v("CI", 8, 24), [[1, 2], [16, 8]])
    iota(v("IOB", 0, HS), [[1, HS]])
    iota(v("IOP", 0, 256), [[1, 16], [16, 16]], 1)
    iota(v("K4", A, 2 * A), [[0, A // 4], [1, 4]])
    for h in range(4):
        keep(v("ET", 512 * h, 512 * h + 512), v("ZERO", 0, 512), [[-4, 128], [-1, 4]], Op.not_equal, 1.0, h, 4)
    line(v("DK", 0, 256), v("N16", 0, 256), HOLD, 0.0)
    for d in range(3):
        keep(v("G16", 0, 272), v("G16" if d else "ZERO", 0, 272), [[-1, 272]], Op.not_equal, 256.0 ** d, 15 + d, 16, group)
    iota(v("G16", 544, 816), [[0, 16], [1, 17]])
    keep(v("G16", 272, 544), v("G16", 544, 816), [[-1, 16], [0, 17]], Op.is_gt, 0.0, 0, 1, group)
    for d, x in enumerate((-4 * HOLD, HOLD)):
        keep(v("G16", 816, 944), v("G16", 816, 944) if d else v("ZERO", 0, 128), [[0, 8], [-1, 16]], Op.not_equal, x, d, 1, group)
    for o, x in ((v("HU", 0, 544), v("G16", 0, 544)), (v("KX", 0, 128), v("G16", 816, 944))):
        dma("s", lambda k, o=o: group(o, k), lambda k, x=x: group(x), [x], [o], 2500, times=8)
    for b in range(6):
        copy(v("HW", 256 * b, 256 * b + 256), v("HU", 15 - 3 * b, 271 - 3 * b))
    ts(v("CI", 1, 2), v("CI", 0, 1), 15, Op.bitwise_and)
    ts(v("CI", 2, 3), v("CI", 0, 1), 2, Op.arith_shift_right, 3, Op.bitwise_and)
    ts(v("CI", 3, 4), v("CI", 0, 1), 3, Op.bitwise_and)
    cp(v("CF", 0, 3), v("CI", 1, 4))
    q, qh, ql, hq, hq4, qh1, h4, hb, hm, h127, q16, q17 = [v("CF", i, i + 1) for i in range(12)]
    JW, PC, KC = v("CF", 16, 32), v("CF", 32, 48), v("CF", 48, 54)
    cp(v("UL", 0, 16), v("CI", 8, 24))
    ts(v("MK", 0, 256), v("N16", 0, 256), q, Op.is_equal)
    line(v("DM", 0, 256), v("MK", 0, 256), -2 * BIG, BIG)
    line(v("KH", 0, 256), v("MK", 0, 256), 3 * BIG, 0.0)
    fill(v("KH", 0, 256, 16), 3 * BIG)
    for o in range(2):
        ts(v("SC", SCW * o, SCW * o + 1), v("ZERO", 0, 1), -HOLD, Op.add)
        cp(v("FL", FLW * o + 257, FLW * (o + 1), 258), v("ZERO", 0, AM))
    fill(v("TB", 0, 1), 0.0)
    ts(hq, q, 15.0, Op.is_lt, -HOLD, Op.mult)
    line(hq4, hq, 4.0, 0.0)
    line(qh1, qh, 1.0, 1.0)
    ts(h4, qh, 3.0, Op.is_lt, -4 * HOLD, Op.mult)
    line(hb, h4, 1.0, ql)
    ts(v("K4", 2 * A, 3 * A), v("K4", A, 2 * A), qh1, Op.is_equal, HOLD, Op.mult)
    ts(v("K4", 3 * A, 4 * A), v("K4", A, 2 * A), qh, Op.is_equal, -4 * HOLD, Op.mult)
    tt(v("K4", 0, A), v("K4", 2 * A, 3 * A), v("K4", 3 * A, 4 * A), Op.add)
    line(hm, hq, 1.0, -1.0)
    line(h127, hq, 1.0, 127.0)
    ts(JW, v("IOB", 0, 256, 16), q, Op.add, -float(HS), Op.add)
    line(q16, q, 16.0, -255.0)
    line(q17, q, 17.0, 0.0)
    line(PC, v("IOB", 0, 16), 1.0, q16)
    ts(KC, v("IOB", 0, A, 16), q, Op.add, h127, Op.subtract)
    quant(v("EQ", 0, 512), v("ES", 0, 512), v("ET", 0, 2048))
    quant(v("UQ", 0, 128), v("US", 0, 128), v("UT", 0, 512))
    for o in range(2):
        ul, up = v("UL", 8 * o, 8 * o + 8), v("UP", 128 * o, 128 * o + 128)
        add("v", cost(up, ind(up, ul)), [v("UQ", 0, 128), ul], [up], lambda ul=ul, up=up: g.vector.tensor_copy(
            ap(up).bitcast(dt.uint32), T.UQ[:, 0:128].bitcast(dt.uint32).indirect(ap(ul))))
        move(v("UPS", 128 * o, 128 * o + 128), ind(v("US", 0, 128), ul))
    quant(v("VQ", 0, 128), v("VS", 0, 128), v("VT", 0, 512))
    l0 = 208 * R
    for t in range(4):
        ts(v("LI", l0 + 16 * t, l0 + 16 * t + 16), v("PT", 0, 16), 4.0, Op.mult, float(t), Op.add)
        move(v("WA", t, 1024, 4), ind(v("M0", 0, 1024), v("LI", l0 + 16 * t, l0 + 16 * t + 16)))
    p16 = v("LI", l0 + 64, l0 + 80)
    cp(p16, v("PT", 0, 16))
    line(v("TW", 0, 1024, 4), ind(v("IOB", 0, 256), p16), 1.0, 1.0)

    def ranks(r, o, out):
        a = ROWS[r][o]
        n = 16 - a
        due[1] = "lay%d" % o
        pv, pa = v("P%d" % (2 * o), 0, 256), v("P%d" % (2 * o + 1), 0, 256)
        side = (v("UP", 128 * o, 128 * o + 128), v("UPS", 128 * o, 128 * o + 128)) + fq(r)
        mm(pa, *side)
        mm(pv, *side)
        z, b, fl, sc, fd = 512 * o, 256 * o, FLW * o, SCW * o, 512 * o
        hf = v("HF", b, b + 256)
        tt(v("D1", b, b + 256), pv, v("DM", 0, 256), Op.max)
        scan(hf, v("KH", 0, 256), v("D1", b, b + 256), Op.add, Op.min)
        m = 16 * n
        act(v("TA", b, b + m), v(pa[0], 0, m), Fn.Abs, bias=2.0 ** -125, scale=1.0625 * 2.0 ** -24)
        act(v("ZZ", z + 16, z + 256), v(pa[0], 16, 256), Fn.Copy)
        tt(v("ZZ", z + 256, z + 256 + m), v(pv[0], 0, m), v("TA", b, b + m), Op.add)
        due[1] = "rows%d" % o
        tt(v("FD", fd, fd + 256), pv, hf, Op.is_equal)
        scan(v("FD", fd + 256, fd + 512), v("DK", 0, 256), v("FD", fd, fd + 256), Op.min, Op.add)
        acc = 512 * r + 16 * o
        for c in range(16):
            win, s = v("ZZ", z + 16 * c + 16, z + 16 * c + 272), v("HF", b + 16 * c + 15, b + 16 * c + 16)
            cut = 16 * c + 16
            if c >= n:
                x = fl + 258 * (c - n)
                ts(v("FL", x, x + cut), v(pv[0], 0, cut), s, Op.is_ge, -0.5, Op.add)
                if cut < 256:
                    ts(v("FL", x + cut, x + 256), v(pv[0], cut, 256), s, Op.is_gt, -0.5, Op.add)
                    together()
            else:
                sg = v("SG", 4096 * o + 256 * c, 4096 * o + 256 * c + 256)
                act(sg, win, Fn.Sign, bias=s, scale=-1.0)
                act(sg, sg, Fn.Relu, scale=-1.0, acc=v("SM", acc + c, acc + c + 1))
        w = 129 * a
        ts(v("FL", fl + 256, fl + 2 * w, 258), v("FD", fd + 256 + m + 15, fd + 512, 16), -1.0, Op.mult, 128.0, Op.add)
        ops[-1]["w"] = [v("FL", x, x + 1) for x in range(fl + 256, fl + 2 * w, 258)]
        due[1] = ("send", "writers")[o]
        flags = [v("FL", fl, fl + 2 * w)]
        scan(v("SC", sc + 1, sc + 1 + w), v("FL", fl, fl + 2 * w, 2), v("FL", fl + 1, fl + 2 * w, 2), Op.add, Op.add, -HOLD)
        ops[-1]["r"] = flags
        tt(v(out[0], out[1] + n, out[2]), v("SC", sc + 129, sc + w + 1, 129), v("SC", sc, sc + w - 128, 129), Op.subtract)
        tt(v(out[0], out[1], out[1] + n), v("SM", acc, acc + n), v("FD", fd + 256 + 15, fd + 256 + m, 16), Op.subtract)

    for r in range(R):
        W, Wn = ("WA", "WB") if r % 2 == 0 else ("WB", "WA")
        tw, tn = TWN * (r % 2), TWN * (1 - r % 2)
        li, sm, ri, wt = 208 * r, 512 * r + 32, 64 * r, PW * r

        def L(a, n):
            return v("LI", li + a, li + a + n)

        def S(a, n):
            return v("SM", sm + a, sm + a + n)

        due[:] = [PERIOD * r, "start"]
        quant(*fq(r), v(W, 0, 1024))
        rho, alp = v("RI", ri, ri + 16), S(432, 16)
        ranks(r, 0, rho)
        cp(L(0, 16), rho)
        cp(ind(v("OF", 0, 256), L(0, 16)), v("IOB", 0, 256))
        hold(v("OM", 128, 160), v("OF", 0, K), "K4")
        ts(L(16, 8), v("OM", 131, 160, 4), 4.0, Op.mult, hb, Op.add)
        move(v("BT", 384, 512), ind(v(W, 0, 1024), L(16, 8)))
        bq, bs = v("BQ", 128 * r, 128 * r + 128), v("BS", 128 * r, 128 * r + 128)
        quant(bq, bs, v("BT", 0, 512))
        lc, ls = fq(r, 0, K)[0], v("FS", SW * r, SW * r + 128)
        oc_, os_ = (lc, ls) if land else (v("RC", K * r, K * r + K), v("RS", 128 * r, 128 * r + 128))
        bc = v("BQ", 128 * r + 128 - K, 128 * r + 128)
        s0 = add("g", 400, [bc, bs], [], lambda r=r, c=(oc_, bc), s=(os_, bs): _hop(
            g, T, topo, core, to, r, (u8(c[0]), u8(c[1])), (ap(s[0]), ap(s[1]))), kind="r")
        i = add("n", 0, [], [lc, ls], None, lat=RING, kind="n", after=[s0])
        ops[i]["round"] = r
        due[1] = "keepers"
        hold(v("OM", 0, 128), v("OF", 0, 128))
        ts(L(24, 8), v("OM", 15, 128, 16), 4.0, Op.mult, hq4, Op.add)
        move(v("TL", 0, 128), ind(v("TW", tw, tw + 1024), L(24, 8)))
        hold(v("TM", 0, 128), v("TL", 0, 128))
        ts(L(160, 8), v("TM", 15, 128, 16), hm, Op.add)
        due[1] = "source"
        ts(v("RI", ri + 16, ri + 32), rho, 159, Op.bitwise_and)
        ts(S(0, 16), v("RI", ri + 16, ri + 32), 4.0, Op.mult, -256.0 - HS, Op.add)
        tt(S(16, 16), S(0, 16), JW, Op.max)
        ts(L(32, 16), S(16, 16), float(HS), Op.add)
        move(v("S1", 0, 256), ind(v("IOB", 0, HS), L(32, 16)))
        ranks(r, 1, alp)
        cp(L(48, 16), alp)
        cp(ind(v("ZF", 0, 256), L(48, 16)), v("S1", 0, 256))
        hold(v("ZM", A, 2 * A), v("ZF", 0, A), "K4")
        ts(L(64, 24), v("ZM", A + 3, 2 * A, 4), 4.0, Op.mult, hb, Op.add)
        ts(S(32, 16), alp, float(A), Op.is_ge, 1000.0, Op.mult)
        act(S(32, 16), alp, Fn.Relu, bias=-1000.0 * (A - 1), scale=1000.0)
        either()
        tt(S(48, 16), alp, S(32, 16), Op.subtract)
        tt(S(64, 16), S(48, 16), S(16, 16), Op.max)
        due[1] = "layer"
        for b in range(4):
            mm(v("P%d" % (4 + b), 0, 128), v("EQ", 128 * b, 128 * b + 128), v("ES", 128 * b, 128 * b + 128), *fq(r, 0, 128))
            move(v(W, 4 * DS + b, 4 * HS, 16), v("P%d" % (4 + b), 0, K))
        for h in range(2):
            move(v("ZT", 192 * h, 192 * h + 192), ind(v(W, 0, 4 * HS), L(64 + 12 * h, 12)))
        quant(v("ZQ", 0, 128), v("ZS", 0, 128), v("ZT", 0, 512))
        for b in range(4):
            mm(v("P%d" % b, 0, 128), v("WC", 128 * b, 128 * b + 128), v("WS", 128 * b, 128 * b + 128),
               v("ZQ", 0, 128), v("ZS", 0, 128))
            line(v("RB", b, 4 * A, 4), v("P%d" % b, 0, A), 0.03125, 0.0, relu=True)
        tt(v(W, 4 * HS, 4 * WN), v("RB", 0, 4 * A), v("ZT", 0, 4 * A), Op.add)
        for t in range(4):
            line(S(368 + 16 * t, 16), S(64, 16), 4.0, float(t + 4 * HS))
        cp(L(96, 64), S(368, 64))
        parts = 2 if r == R - 1 else 1
        for h in range(parts):
            for t in range(4):
                move(v(Wn, 1024 // parts * h + t, 1024 // parts * (h + 1), 4),
                     ind(v(W, 0, 4 * WN), L(96 + 16 * t + 8 * h, 16 // parts)))
        due[1] = "count"
        for b in range(6):
            act(v("HJ", 128 * b, 128 * b + 128), ind(v("HW", 256 * b, 256 * b + 256), L(160, 8)), Fn.Identity,
                acc=S(80 + b, 1))
        due[1] = "free"
        dig, cnt = v("RI", ri + 32, ri + 48), v("RI", ri + 48, ri + 64)
        for d in range(3):
            line(v("SM", sm + 96 + d, sm + 114, 3), S(80, 6), 256.0 ** -d, -0.25)
        cp(dig, S(96, 16))
        ts(cnt, dig, 255, Op.bitwise_and)
        ts(S(128, 16), cnt, 0.0, Op.is_equal)
        scan(S(144, 16), v("IOB", 0, 16), S(128, 16), Op.min, Op.add)
        ts(L(192, 1), S(159, 1), q17, Op.add)
        act(v("HJ", 768, 784), ind(v("HU", 272, 544), L(192, 1)), Fn.Identity, acc=S(224, 1))
        ts(S(248, 16), cnt, 2.0, Op.min, 512.0, Op.mult)
        tt(S(232, 16), S(248, 16), PC, Op.add)
        line(S(264, 16), S(144, 16), 1.0, S(224, 1))
        tt(S(312, 16), S(264, 16), S(232, 16), Op.max)
        ts(L(168, 16), S(312, 16), -1.0, Op.add)
        cp(ind(v("WT", wt + A, wt + PW), L(168, 16)), v("IOP", 0, 256))
        due[1] = "copy"
        move(v("TW", tw + 4 * DS, tw + 4 * HS, 16), v("WT", wt + A, wt + A + K))
        hold(v("ZM", 0, A), v("ZF", 0, A))
        ts(L(88, 6), v("ZM", 15, A, 16), 4.0, Op.mult, hq4, Op.add)
        move(v("WT", wt, wt + A), ind(v("TW", tw, tw + 4 * HS), L(88, 6)))
        hold(v("TF", 0, A), v("WT", wt, wt + A))
        ts(L(184, 6), v("TF", 15, A, 16), hm, Op.add)
        single = ind(v("WT", wt + A + 256, wt + A + 512), L(184, 6))
        ts(v("TB", 1, A + 1), single, 0.0, Op.is_equal, 128.0, Op.mult)
        act(v("TB", 1, A + 1), single, Fn.Relu, bias=128.0, scale=-128.0)
        either()
        line(v("TB", 128, 128 + A), v("TB", 1, A + 1), 129.0 / 128.0, 0.0)
        scan(v("TF", A, 2 * A), v("TB", 128, 128 + A), v("TB", 0, A), Op.add, Op.subtract, -128.0)
        hold(v("TF", 2 * A, 3 * A), v("TF", A, 2 * A))
        tt(S(352, 6), v("TF", 2 * A + 15, 3 * A, 16), KC, Op.max)
        ts(L(200, 6), S(352, 6), h127, Op.add)
        move(v("TW", tw + 4 * HS, tw + TWN, 4), ind(v("WT", wt, wt + A + 128), L(200, 6)))
        if r < R - 1:
            move(v("TW", tn, tn + 1024, 4), ind(v("TW", tw, tw + TWN), L(96, 16)))
        else:
            line(v("TO", 0, 256), ind(v("TW", tw, tw + TWN), L(96, 16)), 1.0, -1.0)
    due[1] = "layer"
    for h in range(2):
        (eq, es), ys = fq(R, K + 128 * h, 128), v("YS", 128 * h, 128 * h + 128)
        quant(eq, es, v("WB" if R % 2 else "WA", 512 * h, 512 * h + 512))
        mm(v("P%d" % (4 + h), 0, 128), v("VQ", 0, 128), v("VS", 0, 128), eq, es)
        move(ys, v("P%d" % (4 + h), 0, 128))
        dma("s", lambda k, h=h: T.oc[:, 512 * h:512 * h + 512], lambda k, x=eq: u8(x), [eq], [], 2100, "st")
        dma("s", lambda k, h=h: T.y[:, 128 * h:128 * h + 128], lambda k, x=ys: ap(x), [ys], [], 2100, "st")
    es = fq(R)[1]
    for k in range(4):
        dma("sa"[k % 2], lambda _, k=k: T.osc[4 * k:4 * k + 4, 0:256],
            lambda _, k=k: T.FS[32 * k:32 * k + 4, es[1]:es[2]], [es], [], 2000, "st")
    dma("s", lambda k: T.om[:], lambda k: T.TO[0:128:16, 0:256], [v("TO", 0, 256)], [], 2000, "st")
    return ops, R * len(topo.engines(core, to[0]))


def rank_program(g, core, T, topo):
    cores = list(T.cores)
    n = len(cores)
    rank = T.rank_of(core)
    if rank is None:
        for i in range(n):
            a, b = cores[i], cores[(i + 1) % n]
            via = _relay(topo, cores, a, b)
            if core not in via:
                continue
            rid, pid = topo.addr(b, core)
            for r in range(R):
                g.wait_ge(T.sem["ac%d" % r], len(topo.engines(a, core)) // 2)
                if core == via[0]:
                    out, in_ = T.FQ[:, CW * r:CW * r + K].bitcast(dt.uint8), T.RC[:, K * r:K * r + K].bitcast(dt.uint8)
                else:
                    out, in_ = T.FS[:, SW * r + 128 - K:SW * r + 128], T.RS[:, 128 * r + 128 - K:128 * r + 128]
                g.remote_dma(out, in_, T.sem["ac%d" % r], T.sem.sent, pid, rid, topo.mask(core, b))
            g.wait_ge(T.sem.sent, R * len(topo.engines(core, b)))
        return
    nxt, prv = cores[(rank + 1) % n], cores[(rank - 1) % n]
    via = _relay(topo, cores, core, nxt)
    frm = _relay(topo, cores, prv, core)
    came = len(topo.engines(prv, core)) if core in frm else sum(len(topo.engines(x, core)) for x in frm)
    ops, sent = _calls(g, T, via, topo, core, nxt in via)
    deps, (_, order, way, at) = _plan(ops)
    queue = {"v": g.vector, "a": g.scalar, "t": g.tensor, "g": g, "s": g.sync}
    count = {"v": 0, "a": 0, "t": 0, "g": 0, "st": 0}
    known = {q: {} for q in queue}
    for i in order:
        o = ops[i]
        q, _, emit = o["ways"][way[i]]
        if o["kind"] == "n":
            o["done"] = {"ac%d" % o["round"]: came}
            o["knew"] = {}
            continue
        kn, need = known[q], {}
        for j in deps[i]:
            for s, c in ops[j]["done"].items():
                if kn.get(s, 0) < c and need.get(s, (0, 0))[0] < c:
                    need[s] = (c, j)
        for s in sorted(need, key=lambda s: -at[need[s][1]]):
            c, j = need[s]
            if kn.get(s, 0) >= c:
                continue
            queue[q].wait_ge(T.sem[s], c)
            kn[s] = c
            for s2, c2 in ops[j]["knew"].items():
                kn[s2] = max(kn.get(s2, 0), c2)
        o["knew"] = dict(kn)
        ins = emit()
        if o["kind"] == "r":
            o["done"] = {}
        elif o["kind"] == "d":
            for x in ins:
                x.then_inc(T.sem[o["sem"]], 16)
            count[o["sem"]] = count.get(o["sem"], 0) + 16 * len(ins)
            o["done"] = {o["sem"]: count[o["sem"]]}
        else:
            for x in ins if isinstance(ins, list) else [ins]:
                count[q] += 1
                x.then_inc(T.sem[q], 1)
            o["done"] = {q: count[q]}
    for s in count:
        g.wait_ge(T.sem[s], count[s])
    g.wait_ge(T.sem.sent, sent)
